import numpy as np
import ml_dtypes


def mxq(x, axis, fmt="e4m3"):
    dtype, down = {"e4m3": (ml_dtypes.float8_e4m3fn, 7), "e5m2": (ml_dtypes.float8_e5m2, 14)}[fmt]
    v = np.moveaxis(np.asarray(x, np.float32).astype(ml_dtypes.bfloat16).astype(np.float64), axis, -1)
    blocks = v.reshape(v.shape[:-1] + (-1, 32))
    amax = np.abs(blocks).max(-1, keepdims=True)
    byte = np.maximum(np.where(amax > 0, np.frexp(amax)[1] - 1 + 127, 0) - down, 1)
    scale = np.exp2(byte - 127.0)
    codes = (blocks / scale).astype(np.float32).astype(dtype).astype(np.float64)
    return np.moveaxis((codes * scale).reshape(v.shape), -1, axis)


WIDE = False


def mx_kscale(k):
    if not WIDE:
        return np.ones(k)
    levels = np.array([10, -10, 5, -5, 0])
    if k % 512:
        return np.exp2(np.random.permutation(np.resize(levels, k // 32))).repeat(32)
    a = np.empty((k // 512, 16))
    for p in range(k // 512):
        a[p, :8] = np.random.permutation(np.resize(levels, 8))
        for g in range(8):
            far = levels[np.abs(levels - a[p, g]) >= 10]
            a[p, g + 8] = far[np.random.randint(len(far))]
    return np.exp2(a.ravel()).repeat(32)


def f64(x):
    return np.asarray(x).astype(np.float64)


def striped(idx):
    return np.tile(idx.reshape(-1, 16).T, (8, 1)).astype(np.uint16)


def unstriped(offs):
    return offs[:16].T.reshape(-1).astype(np.int64)


E2M1 = np.array([0.0, 0.5, 1.0, 1.5, 2.0, 3.0, 4.0, 6.0, -0.0, -0.5, -1.0, -1.5, -2.0, -3.0, -4.0, -6.0])


def pack_weight(w, fmt):
    k, n = w.shape
    w = f64(np.asarray(w, np.float32).astype(ml_dtypes.bfloat16)).reshape(k // 32, 32, n)
    amax = np.abs(w).max(1)
    if fmt == "e4m3":
        byte = np.frexp(amax)[1] - 1 + 127 - 7
    else:
        mant, ex = np.frexp(amax / 6.0)
        byte = np.where(mant > 0.5, ex, ex - 1) + 127
    byte = np.clip(np.where(amax > 0, byte, 1), 1, 254)
    scaled = (w * np.exp2(127.0 - byte)[:, None, :]).reshape(k, n).astype(np.float32)
    by_word = np.ascontiguousarray(scaled.reshape(k // 512, 128, 4, n).transpose(0, 1, 3, 2))
    if fmt == "e4m3":
        words = by_word.astype(ml_dtypes.float8_e4m3fn).view(np.uint8)
    else:
        c = by_word.astype(ml_dtypes.float4_e2m1fn).view(np.uint8) & 0xF
        words = (c[..., 0::2] | (c[..., 1::2] << 4)).reshape(k // 512, 128, 2 * n)
    return np.ascontiguousarray(words), np.ascontiguousarray(byte.astype(np.uint8).reshape(k // 512, 16, n))


def unpack_weight(words, scales, fmt):
    g, _, n = scales.shape
    words = np.ascontiguousarray(words).reshape(g, 128, n, -1)
    if fmt == "e4m3":
        vals = words.view(ml_dtypes.float8_e4m3fn).astype(np.float64)
    else:
        nib = np.empty((g, 128, n, 4), np.uint8)
        nib[..., 0::2] = words & 0xF
        nib[..., 1::2] = words >> 4
        vals = E2M1[nib]
    vals = vals * np.repeat(np.exp2(scales.astype(np.float64) - 127.0), 8, axis=1)[..., None]
    return vals.transpose(0, 1, 3, 2).reshape(g * 512, n)


def silu(v):
    return v / (1.0 + np.exp(-np.maximum(v, -700.0)))


K, T, E, C, N = 512, 384, 6, 128, 512


def by_expert(wq, xq):
    return np.concatenate([wq[e].T @ xq[:, e * C:(e + 1) * C] for e in range(E)], axis=1)


def setup_inputs():
    n = np.random.standard_normal
    s = mx_kscale(K)[:, None]
    first = np.random.permutation(np.repeat(np.arange(E), T // E))
    second = (first + 1 + np.random.permutation(np.repeat(np.arange(E - 1), -(-T // (E - 1)))[:T])) % E
    while np.bincount(second, minlength=E).max() != T // E:
        load = np.bincount(second, minlength=E); hi, lo = int(load.argmax()), int(load.argmin())
        t = np.flatnonzero((second == hi) & (first != lo))[0]; second[t] = lo
    slot_token = np.empty(E * C, np.int64); pos = np.empty((2, T), np.int64); fill = np.zeros(E, np.int64)
    place = np.stack([np.random.permutation(C) for _ in range(E)])
    for r, deal in enumerate((first, second)):
        for t in np.random.permutation(T):
            e = deal[t]; j = e * C + place[e, fill[e]]; fill[e] += 1; slot_token[j] = t; pos[r, t] = j
    g = np.random.uniform(0.2, 0.8, T)
    w = [pack_weight(m, "e2m1") for m in n((E + 1, K, N)) / np.sqrt(K) / s[None]]
    return {
        "xT": (n((K, T)) * s).astype(np.float32),
        "w_words": np.stack([m[0] for m in w]),
        "w_scales": np.stack([m[1] for m in w]),
        "b": (0.3 * n((N, E + 1))).astype(np.float32),
        "gate": np.stack([np.tile(g, (N, 1)), np.tile(1.0 - g, (N, 1))]).astype(np.float32),
        "offs": striped(slot_token),
        "pos1": striped(pos[0]),
        "pos2": striped(pos[1]),
    }


def reference(xT, w_words, w_scales, b, gate, offs, pos1, pos2):
    idx = unstriped(offs)
    w = np.stack([unpack_weight(w_words[e], w_scales[e], "e2m1") for e in range(E + 1)])
    wq = w
    xs = mxq(f64(xT), 0, "e4m3")
    ys = silu((wq[E].T @ xs) + f64(b)[:, E:])
    xq = mxq(f64(xT)[:, idx], 0, "e4m3")
    y = by_expert(w, xq)
    y = silu(y + np.repeat(f64(b)[:, :E], C, axis=1))
    return ys + f64(gate[0]) * y[:, unstriped(pos1)] + f64(gate[1]) * y[:, unstriped(pos2)]

@@ -1,0 +1,226 @@
+import concourse.mybir as mybir
+from contextlib import ExitStack
+
+K, T, E, C, N = 512, 384, 6, 128, 512
+S = E * C
+P = 128
+M_TILES = N // P
+
+F32 = mybir.dt.float32
+BF16 = mybir.dt.bfloat16
+I32 = mybir.dt.int32
+U32 = mybir.dt.uint32
+U16 = mybir.dt.uint16
+U8 = mybir.dt.uint8
+FP8X4 = mybir.dt.float8_e4m3fn_x4
+FP4X4 = mybir.dt.float4_e2m1fn_x4
+
+MULT = mybir.AluOpType.mult
+ADD = mybir.AluOpType.add
+SILU = mybir.ActivationFunctionType.Silu
+COPY = mybir.ActivationFunctionType.Copy
+
+FLOPS = 2 * K * N * (S + T)
+BYTES = 4 * K * T + (E + 1) * (K * N // 2 + K * N // 32) + 4 * N * (E + 1) + 2 * 4 * T + 2 * 128 * (48 + 24 + 24) + 4 * N * T
+
+WINDOW = 512
+
+
+def tile_moe_shr_lin_silu_kernel(tc, xT, w_words, w_scales, b, gate, offs, pos1, pos2, out):
+    nc = tc.nc
+    with ExitStack() as ctx:
+        lists = ctx.enter_context(tc.tile_pool(name="lists", bufs=1))
+        keep = ctx.enter_context(tc.tile_pool(name="keep", bufs=1))
+        psum = ctx.enter_context(tc.psum_pool(name="psum", bufs=8))
+
+        offs_t = lists.tile([P, S // 16], U16, name="offs_t")
+        pos1_t = lists.tile([P, T // 16], U16, name="pos1_t")
+        pos2_t = lists.tile([P, T // 16], U16, name="pos2_t")
+
+        raw = keep.tile([P, 4, T], F32, name="raw")
+        pairs = [keep.tile([P, 2 * WINDOW], BF16, name=f"pairs{u}", align_bytes=64) for u in range(2)]
+        rows = keep.tile([P, 5 * WINDOW], BF16, name="rows", align_bytes=64)
+        words = [keep.tile([P, (E + 1) * N], U8, name=f"words{h}", align_bytes=64) for h in range(2)]
+        scales_w = [keep.tile([P, (E + 1) * N // 2], U8, name=f"scales_w{h}", align_bytes=64) for h in range(2)]
+        bias = keep.tile([P, M_TILES, E + 1], F32, name="bias")
+        dummy = keep.tile([P, 1], F32, name="dummy")
+        gates = [keep.tile([P, 2, T], F32, name=f"gates{m}") for m in range(M_TILES)]
+
+        x_rows = xT.rearrange("(p j) t -> p j t", j=4)
+        nc.sync.dma_start(raw[:, 0:2], x_rows[:, 0:2])
+        nc.sync.dma_start(offs_t[:], offs)
+        nc.sync.dma_start(raw[:, 2:4], x_rows[:, 2:4])
+
+        for h in range(2):
+            nc.vector.memset(scales_w[h][:].bitcast(I32), 0)
+        nc.gpsimd.memset(dummy[:], 0.0)
+        nc.scalar.activation(dummy[:], dummy[:], SILU)
+        for u in range(2):
+            nc.gpsimd.memset(pairs[u][:, 2 * T :], 0.0)
+        row_of = rows[:].rearrange("p (r t) -> p r t", t=WINDOW)
+        nc.gpsimd.memset(row_of[:, 0:4, T:], 0.0)
+        nc.gpsimd.memset(row_of[:, 4], 0.0)
+        place = (0, 2, 1, 3)
+
+        w_scales_i = w_scales.bitcast(I32)
+        w_i = w_words.bitcast(I32)
+
+        def load_weights(h):
+            nc.sync.dma_start(
+                words[h][:].bitcast(I32).rearrange("p (e c) -> p e c", e=E + 1),
+                w_i[:, 0, :, h * N // 4 : (h + 1) * N // 4].rearrange("e p c -> p e c"),
+            )
+            for q in range(4):
+                nc.sync.dma_start(
+                    scales_w[h][:].bitcast(I32).rearrange("p (e c) -> p e c", e=E + 1)[32 * q : 32 * q + 4],
+                    w_scales_i[:, 0, 4 * q : 4 * q + 4, h * N // 8 : (h + 1) * N // 8].rearrange("e q c -> q e c"),
+                )
+
+        def load_gates(m):
+            nc.sync.dma_start(gates[m][:], gate[:, m * P : (m + 1) * P, :].rearrange("r p t -> p r t"))
+
+        load_weights(0)
+        nc.sync.dma_start(bias[:], b.rearrange("(m p) e -> p m e", p=P))
+        load_gates(0)
+        nc.sync.dma_start(pos1_t[:], pos1)
+        nc.sync.dma_start(pos2_t[:], pos2)
+        load_weights(1)
+        for m in range(1, M_TILES):
+            load_gates(m)
+
+        def cast(engine_copy, u, t0, t1):
+            engine_copy(
+                pairs[u][:, 2 * t0 : 2 * t1].rearrange("p (t e) -> p t e", e=2),
+                raw[:, 2 * u : 2 * u + 2, t0:t1].rearrange("p e t -> p t e"),
+            )
+
+        def lhsT(e, m):
+            col = e * N // 2 + m % 2 * P
+            return dict(
+                lhsT=words[m // 2][:, 2 * col : 2 * (col + P)].bitcast(FP4X4),
+                lhsT_scale=scales_w[m // 2][:, col : col + P],
+            )
+
+        windows = [pairs[u][:].bitcast(U32) for u in range(2)]
+        spans = ((0, 5 * C), (5 * C, S), (S, S + T))
+        picked = [keep.tile([P, s1 - s0, 4], BF16, name=f"picked{s0}", align_bytes=64) for s0, s1 in spans]
+        codes = [keep.tile([P, s1 - s0], U32, name=f"codes{s0}", align_bytes=64) for s0, s1 in spans]
+        scales = [keep.tile([P, s1 - s0], U8, name=f"scales{s0}", align_bytes=64) for s0, s1 in spans]
+        CUTS = ((0, 384), (384, 640))
+        planes = [keep.tile([P, 2, 2 * (s1 - s0)], BF16, name=f"planes{s0}", align_bytes=64) for s0, s1 in CUTS]
+
+        def pick_pairs(i, u):
+            s0, s1 = CUTS[i]
+            nc.vector.tensor_copy(planes[i][:, u].bitcast(U32), windows[u].indirect(offs_t[:, s0 // 16 : s1 // 16]))
+
+        def interleave(i):
+            s0, s1 = CUTS[i]
+            nc.vector.tensor_copy(
+                picked[0][:, s0:s1].rearrange("p s j -> p (s j)").bitcast(I32).rearrange("p (s u) -> p s u", u=2),
+                planes[i][:].rearrange("p u c -> p (u c)").bitcast(I32).rearrange("p (u s) -> p s u", u=2),
+            )
+
+        def pick_row(e, j):
+            nc.scalar.activation(
+                picked[1][:, :, j],
+                rows[:, place[j] * WINDOW : (place[j] + 2) * WINDOW].indirect(offs_t[:, e * C // 16 : (e + 1) * C // 16]),
+                COPY,
+            )
+
+        def quantise(i, s0, s1):
+            nc.vector.quantize_mx(
+                out=codes[i][:, s0:s1].bitcast(FP8X4),
+                scales=scales[i][:, s0:s1],
+                in_=picked[i][:, s0:s1].rearrange("p s j -> p (s j)"),
+            )
+
+        cast(nc.vector.tensor_copy, 0, 0, T)
+        nc.scalar.copy(row_of[:, 0:4:2, 0:T], raw[:, 0:2])
+        cast(nc.scalar.copy, 1, 0, T)
+        nc.scalar.copy(row_of[:, 1:4:2, 0:T], raw[:, 2:4])
+        for i in range(2):
+            pick_pairs(i, 0)
+        for j in range(4):
+            pick_row(5, j)
+        for t0, t1 in ((0, 128), (128, 256), (256, T)):
+            nc.gpsimd.tensor_scalar(
+                picked[2][:, t0:t1], raw[:, :, t0:t1].rearrange("p j t -> p t j"), 1.0, 0.0, MULT, ADD
+            )
+        for i in range(2):
+            pick_pairs(i, 1)
+        for i in range(2):
+            interleave(i)
+        for i, s0, s1 in ((0, 0, 256), (0, 256, 512), (0, 512, 640), (1, 0, 128), (2, 0, 256), (2, 256, 384)):
+            quantise(i, s0, s1)
+
+        y = [keep.tile([P, S], F32, name=f"y{m}") for m in range(M_TILES)]
+        ys = [keep.tile([P, 2, T], F32, name=f"ys{m}") for m in range(2)]
+
+        def product(sums, e, m, s0, s1):
+            i = [j for j in range(3) if spans[j][0] <= s0 < spans[j][1]][0]
+            s0, s1 = s0 - spans[i][0], s1 - spans[i][0]
+            nc.tensor.matmul_mx(
+                out=sums,
+                rhs=codes[i][:, s0:s1].bitcast(FP8X4),
+                rhs_scale=scales[i][:, s0:s1],
+                start=True,
+                stop=True,
+                **lhsT(e, m),
+            )
+
+        for m in range(M_TILES):
+            for e0 in (0, 2, 4):
+                sums = psum.tile([P, 2, C], F32, name="sums")
+                for e in (e0, e0 + 1):
+                    product(sums[:, e - e0], e, m, e * C, (e + 1) * C)
+                for e in (e0, e0 + 1):
+                    nc.scalar.activation(
+                        y[m][:, e * C : (e + 1) * C], sums[:, e - e0], SILU, bias=bias[:, m, e : e + 1]
+                    )
+            sums = psum.tile([P, T], F32, name="sums")
+            for t0, t1 in ((0, 256), (256, T)):
+                product(sums[:, t0:t1], E, m, S + t0, S + t1)
+            nc.scalar.activation(ys[m // 2][:, m % 2], sums[:], SILU, bias=bias[:, m, E : E + 1])
+
+        first = [keep.tile([P, 2, T], F32, name=f"first{m}") for m in range(2)]
+        second = [keep.tile([P, 2, T], F32, name=f"second{m}") for m in range(2)]
+        part = [keep.tile([P, 2, T], F32, name=f"part{m}") for m in range(2)]
+        total = [keep.tile([P, 2, T], F32, name=f"total{m}") for m in range(2)]
+
+        def gather(to, m, listed, r, t0=0, t1=T):
+            nc.vector.tensor_tensor(
+                to[m // 2][:, m % 2, t0:t1],
+                y[m][:].indirect(listed[:, t0 // 16 : t1 // 16]),
+                gates[m][:, r, t0:t1],
+                MULT,
+            )
+
+        def add(to, a, b, m, span, t0=0, t1=T):
+            at = (slice(None), slice(m % 2, m % 2 + span), slice(t0, t1))
+            nc.vector.tensor_tensor(to[m // 2][at], a[m // 2][at], b[m // 2][at], ADD)
+
+        def store(m, t0=0, t1=T):
+            nc.sync.dma_start(out[m * P : (m + 1) * P, t0:t1], total[m // 2][:, m % 2, t0:t1])
+
+        gather(first, 0, pos1_t, 0)
+        gather(second, 0, pos2_t, 1)
+        gather(first, 1, pos1_t, 0)
+        gather(second, 1, pos2_t, 1)
+        add(part, ys, first, 0, 2)
+        gather(first, 2, pos1_t, 0)
+        add(total, part, second, 0, 2)
+        store(0)
+        store(1)
+        gather(second, 2, pos2_t, 1)
+        add(part, ys, first, 2, 1)
+        gather(first, 3, pos1_t, 0)
+        add(total, part, second, 2, 1)
+        store(2)
+        LATE = 256
+        gather(second, 3, pos2_t, 1, 0, LATE)
+        add(part, ys, first, 3, 1)
+        gather(second, 3, pos2_t, 1, LATE, T)
+        add(total, part, second, 3, 1, 0, LATE)
+        store(3, 0, LATE)
+        add(total, part, second, 3, 1, LATE, T)
+        store(3, LATE, T)

@@ -1,4 +1,5 @@
 import concourse.mybir as mybir
+from concourse.masks import make_identity
 from contextlib import ExitStack
 
 K, T, E, C, N = 512, 384, 6, 128, 512
@@ -31,7 +32,7 @@ def tile_moe_shr_lin_silu_kernel(tc, xT, w_words, w_scales, b, gate, offs, pos1,
     with ExitStack() as ctx:
         lists = ctx.enter_context(tc.tile_pool(name="lists", bufs=1))
         keep = ctx.enter_context(tc.tile_pool(name="keep", bufs=1))
-        psum = ctx.enter_context(tc.psum_pool(name="psum", bufs=8))
+        psum = ctx.enter_context(tc.psum_pool(name="psum", bufs=1))
 
         offs_t = lists.tile([P, S // 16], U16, name="offs_t")
         pos1_t = lists.tile([P, T // 16], U16, name="pos1_t")
@@ -44,7 +45,7 @@ def tile_moe_shr_lin_silu_kernel(tc, xT, w_words, w_scales, b, gate, offs, pos1,
         scales_w = [keep.tile([P, (E + 1) * N // 2], U8, name=f"scales_w{h}", align_bytes=64) for h in range(2)]
         bias = keep.tile([P, M_TILES, E + 1], F32, name="bias")
         dummy = keep.tile([P, 1], F32, name="dummy")
-        gates = [keep.tile([P, 2, T], F32, name=f"gates{m}") for m in range(M_TILES)]
+        gates = keep.tile([P, 2, T], F32, name="gates")
 
         x_rows = xT.rearrange("(p j) t -> p j t", j=4)
         nc.sync.dma_start(raw[:, 0:2], x_rows[:, 0:2])
@@ -61,6 +62,8 @@ def tile_moe_shr_lin_silu_kernel(tc, xT, w_words, w_scales, b, gate, offs, pos1,
         nc.gpsimd.memset(row_of[:, 0:4, T:], 0.0)
         nc.gpsimd.memset(row_of[:, 4], 0.0)
         place = (0, 2, 1, 3)
+        identity = keep.tile([P, P], F32, name="identity")
+        make_identity(nc, identity[:])
 
         w_scales_i = w_scales.bitcast(I32)
         w_i = w_words.bitcast(I32)
@@ -76,17 +79,12 @@ def tile_moe_shr_lin_silu_kernel(tc, xT, w_words, w_scales, b, gate, offs, pos1,
                     w_scales_i[:, 0, 4 * q : 4 * q + 4, h * N // 8 : (h + 1) * N // 8].rearrange("e q c -> q e c"),
                 )
 
-        def load_gates(m):
-            nc.sync.dma_start(gates[m][:], gate[:, m * P : (m + 1) * P, :].rearrange("r p t -> p r t"))
-
         load_weights(0)
         nc.sync.dma_start(bias[:], b.rearrange("(m p) e -> p m e", p=P))
-        load_gates(0)
+        nc.sync.dma_start(gates[:], gate[:, 0:P, :].rearrange("r p t -> p r t"))
         nc.sync.dma_start(pos1_t[:], pos1)
         nc.sync.dma_start(pos2_t[:], pos2)
         load_weights(1)
-        for m in range(1, M_TILES):
-            load_gates(m)
 
         def cast(engine_copy, u, t0, t1):
             engine_copy(
@@ -154,7 +152,14 @@ def tile_moe_shr_lin_silu_kernel(tc, xT, w_words, w_scales, b, gate, offs, pos1,
             quantise(i, s0, s1)
 
         y = [keep.tile([P, S], F32, name=f"y{m}") for m in range(M_TILES)]
-        ys = [keep.tile([P, 2, T], F32, name=f"ys{m}") for m in range(2)]
+        ys = [keep.tile([P, T], F32, name=f"ys{m}") for m in range(M_TILES)]
+        first = [keep.tile([P, T], F32, name=f"first{m}") for m in range(M_TILES)]
+        second = [keep.tile([P, T], F32, name=f"second{m}") for m in range(M_TILES)]
+        part = [keep.tile([P, T], F32, name=f"part{m}") for m in range(M_TILES)]
+        total = [keep.tile([P, T], F32, name=f"total{m}") for m in range(M_TILES)]
+
+        def bank(i):
+            return psum.tile([P, 512], F32, name=f"bank{i}")
 
         def product(sums, e, m, s0, s1):
             i = [j for j in range(3) if spans[j][0] <= s0 < spans[j][1]][0]
@@ -168,59 +173,85 @@ def tile_moe_shr_lin_silu_kernel(tc, xT, w_words, w_scales, b, gate, offs, pos1,
                 **lhsT(e, m),
             )
 
-        for m in range(M_TILES):
-            for e0 in (0, 2, 4):
-                sums = psum.tile([P, 2, C], F32, name="sums")
-                for e in (e0, e0 + 1):
-                    product(sums[:, e - e0], e, m, e * C, (e + 1) * C)
-                for e in (e0, e0 + 1):
+        def routed(m):
+            for i, experts in enumerate((range(0, 4), range(4, E))):
+                sums = bank(2 * m + i)
+                for e in experts:
+                    product(sums[:, e % 4 * C : (e % 4 + 1) * C], e, m, e * C, (e + 1) * C)
+                for e in experts:
                     nc.scalar.activation(
-                        y[m][:, e * C : (e + 1) * C], sums[:, e - e0], SILU, bias=bias[:, m, e : e + 1]
+                        y[m][:, e * C : (e + 1) * C],
+                        sums[:, e % 4 * C : (e % 4 + 1) * C],
+                        SILU,
+                        bias=bias[:, m, e : e + 1],
                     )
-            sums = psum.tile([P, T], F32, name="sums")
+
+        def shared(m):
+            sums = bank(m)
             for t0, t1 in ((0, 256), (256, T)):
                 product(sums[:, t0:t1], E, m, S + t0, S + t1)
-            nc.scalar.activation(ys[m // 2][:, m % 2], sums[:], SILU, bias=bias[:, m, E : E + 1])
-
-        first = [keep.tile([P, 2, T], F32, name=f"first{m}") for m in range(2)]
-        second = [keep.tile([P, 2, T], F32, name=f"second{m}") for m in range(2)]
-        part = [keep.tile([P, 2, T], F32, name=f"part{m}") for m in range(2)]
-        total = [keep.tile([P, 2, T], F32, name=f"total{m}") for m in range(2)]
+            nc.scalar.activation(ys[m][:], sums[:, 0:T], SILU, bias=bias[:, m, E : E + 1])
 
         def gather(to, m, listed, r, t0=0, t1=T):
             nc.vector.tensor_tensor(
-                to[m // 2][:, m % 2, t0:t1],
-                y[m][:].indirect(listed[:, t0 // 16 : t1 // 16]),
-                gates[m][:, r, t0:t1],
-                MULT,
+                to[m][:, t0:t1], y[m][:].indirect(listed[:, t0 // 16 : t1 // 16]), gates[:, r, t0:t1], MULT
             )
 
-        def add(to, a, b, m, span, t0=0, t1=T):
-            at = (slice(None), slice(m % 2, m % 2 + span), slice(t0, t1))
-            nc.vector.tensor_tensor(to[m // 2][at], a[m // 2][at], b[m // 2][at], ADD)
+        def add(to, a, b, m, t0=0, t1=T):
+            nc.vector.tensor_tensor(to[m][:, t0:t1], a[m][:, t0:t1], b[m][:, t0:t1], ADD)
 
         def store(m, t0=0, t1=T):
-            nc.sync.dma_start(out[m * P : (m + 1) * P, t0:t1], total[m // 2][:, m % 2, t0:t1])
+            nc.sync.dma_start(out[m * P : (m + 1) * P, t0:t1], total[m][:, t0:t1])
 
-        gather(first, 0, pos1_t, 0)
-        gather(second, 0, pos2_t, 1)
-        gather(first, 1, pos1_t, 0)
-        gather(second, 1, pos2_t, 1)
-        add(part, ys, first, 0, 2)
-        gather(first, 2, pos1_t, 0)
-        add(total, part, second, 0, 2)
-        store(0)
-        store(1)
-        gather(second, 2, pos2_t, 1)
-        add(part, ys, first, 2, 1)
-        gather(first, 3, pos1_t, 0)
-        add(total, part, second, 2, 1)
-        store(2)
+        def turn_and_add(m, i):
+            sums = bank(i)
+            terms = (ys, first, second)
+            for t0 in range(0, T, P):
+                for j, term in enumerate(terms):
+                    nc.tensor.matmul(
+                        sums[:, t0 : t0 + P],
+                        lhsT=term[m][:, t0 : t0 + P],
+                        rhs=identity[:],
+                        is_transpose=True,
+                        start=j == 0,
+                        stop=j == len(terms) - 1,
+                    )
+            nc.scalar.copy(part[m][:], sums[:, 0:T])
+
+        def turn_back(m, i):
+            sums = bank(i)
+            for t0 in range(0, T, P):
+                nc.tensor.transpose(sums[:, t0 : t0 + P], part[m][:, t0 : t0 + P], identity[:])
+            nc.scalar.copy(total[m][:], sums[:, 0:T])
+            store(m)
+
+        def gathers(m):
+            gather(first, m, pos1_t, 0)
+            gather(second, m, pos2_t, 1)
+
+        routed(0)
+        routed(1)
+        gathers(0)
+        shared(0)
+        routed(2)
+        gathers(1)
+        shared(1)
+        routed(3)
+        gathers(2)
+        shared(2)
+        shared(3)
+        turn_and_add(0, 4)
+        turn_back(0, 5)
+        turn_and_add(1, 6)
+        turn_back(1, 7)
+        turn_and_add(2, 0)
+        turn_back(2, 1)
         LATE = 256
+        gather(first, 3, pos1_t, 0)
         gather(second, 3, pos2_t, 1, 0, LATE)
-        add(part, ys, first, 3, 1)
+        add(part, ys, first, 3)
         gather(second, 3, pos2_t, 1, LATE, T)
-        add(total, part, second, 3, 1, 0, LATE)
+        add(total, part, second, 3, 0, LATE)
         store(3, 0, LATE)
-        add(total, part, second, 3, 1, LATE, T)
+        add(total, part, second, 3, LATE, T)
         store(3, LATE, T)

@@ -19,7 +19,6 @@ FP4X4 = mybir.dt.float4_e2m1fn_x4
 MULT = mybir.AluOpType.mult
 ADD = mybir.AluOpType.add
 SILU = mybir.ActivationFunctionType.Silu
-COPY = mybir.ActivationFunctionType.Copy
 
 FLOPS = 2 * K * N * (S + T)
 BYTES = 4 * K * T + (E + 1) * (K * N // 2 + K * N // 32) + 4 * N * (E + 1) + 2 * 4 * T + 2 * 128 * (48 + 24 + 24) + 4 * N * T
@@ -39,8 +38,7 @@ def tile_moe_shr_lin_silu_kernel(tc, xT, w_words, w_scales, b, gate, offs, pos1,
         pos2_t = lists.tile([P, T // 16], U16, name="pos2_t")
 
         raw = keep.tile([P, 4, T], F32, name="raw")
-        pairs = [keep.tile([P, 2 * WINDOW], BF16, name=f"pairs{u}", align_bytes=64) for u in range(2)]
-        rows = keep.tile([P, 5 * WINDOW], BF16, name="rows", align_bytes=64)
+        pairs = keep.tile([P, 4 * WINDOW], BF16, name="pairs", align_bytes=64)
         words = [keep.tile([P, (E + 1) * N], U8, name=f"words{h}", align_bytes=64) for h in range(2)]
         scales_w = [keep.tile([P, (E + 1) * N // 2], U8, name=f"scales_w{h}", align_bytes=64) for h in range(2)]
         bias = keep.tile([P, M_TILES, E + 1], F32, name="bias")
@@ -57,11 +55,7 @@ def tile_moe_shr_lin_silu_kernel(tc, xT, w_words, w_scales, b, gate, offs, pos1,
         nc.gpsimd.memset(dummy[:], 0.0)
         nc.scalar.activation(dummy[:], dummy[:], SILU)
         for u in range(2):
-            nc.gpsimd.memset(pairs[u][:, 2 * T :], 0.0)
-        row_of = rows[:].rearrange("p (r t) -> p r t", t=WINDOW)
-        nc.gpsimd.memset(row_of[:, 0:4, T:], 0.0)
-        nc.gpsimd.memset(row_of[:, 4], 0.0)
-        place = (0, 2, 1, 3)
+            nc.gpsimd.memset(pairs[:, 2 * (u * WINDOW + T) : 2 * (u + 1) * WINDOW], 0.0)
         identity = keep.tile([P, P], F32, name="identity")
         make_identity(nc, identity[:])
 
@@ -88,7 +82,7 @@ def tile_moe_shr_lin_silu_kernel(tc, xT, w_words, w_scales, b, gate, offs, pos1,
 
         def cast(engine_copy, u, t0, t1):
             engine_copy(
-                pairs[u][:, 2 * t0 : 2 * t1].rearrange("p (t e) -> p t e", e=2),
+                pairs[:, 2 * (u * WINDOW + t0) : 2 * (u * WINDOW + t1)].rearrange("p (t e) -> p t e", e=2),
                 raw[:, 2 * u : 2 * u + 2, t0:t1].rearrange("p e t -> p t e"),
             )
 
@@ -99,57 +93,52 @@ def tile_moe_shr_lin_silu_kernel(tc, xT, w_words, w_scales, b, gate, offs, pos1,
                 lhsT_scale=scales_w[m // 2][:, col : col + P],
             )
 
-        windows = [pairs[u][:].bitcast(U32) for u in range(2)]
-        spans = ((0, 5 * C), (5 * C, S), (S, S + T))
-        picked = [keep.tile([P, s1 - s0, 4], BF16, name=f"picked{s0}", align_bytes=64) for s0, s1 in spans]
-        codes = [keep.tile([P, s1 - s0], U32, name=f"codes{s0}", align_bytes=64) for s0, s1 in spans]
+        windows = [pairs[:].bitcast(U32)[:, u * WINDOW : (u + 1) * WINDOW] for u in range(2)]
+        spans = ((0, 2 * C), (2 * C, 4 * C), (4 * C, S), (S, S + T))
+        codes = [keep.tile([P, s1 - s0], U32, name=f"codes{s0}", align_bytes=64) for s0, s1 in spans[:3]]
         scales = [keep.tile([P, s1 - s0], U8, name=f"scales{s0}", align_bytes=64) for s0, s1 in spans]
-        CUTS = ((0, 384), (384, 640))
-        planes = [keep.tile([P, 2, 2 * (s1 - s0)], BF16, name=f"planes{s0}", align_bytes=64) for s0, s1 in CUTS]
+        planes = keep.tile([P, 2 * S], U32, name="planes", align_bytes=64)
+        picked = [
+            keep.tile([P, 2 * (s1 - s0)], U32, name="last_picked" if s1 == S else f"picked{s0}", align_bytes=64)[:]
+            for s0, s1 in spans
+        ]
 
-        def pick_pairs(i, u):
-            s0, s1 = CUTS[i]
-            nc.vector.tensor_copy(planes[i][:, u].bitcast(U32), windows[u].indirect(offs_t[:, s0 // 16 : s1 // 16]))
-
-        def interleave(i):
-            s0, s1 = CUTS[i]
+        def pick_pairs(u, s0, s1):
             nc.vector.tensor_copy(
-                picked[0][:, s0:s1].rearrange("p s j -> p (s j)").bitcast(I32).rearrange("p (s u) -> p s u", u=2),
-                planes[i][:].rearrange("p u c -> p (u c)").bitcast(I32).rearrange("p (u s) -> p s u", u=2),
+                planes[:, u * S + s0 : u * S + s1], windows[u].indirect(offs_t[:, s0 // 16 : s1 // 16])
             )
 
-        def pick_row(e, j):
-            nc.scalar.activation(
-                picked[1][:, :, j],
-                rows[:, place[j] * WINDOW : (place[j] + 2) * WINDOW].indirect(offs_t[:, e * C // 16 : (e + 1) * C // 16]),
-                COPY,
+        def interleave(i):
+            s0, s1 = spans[i]
+            nc.scalar.copy(
+                picked[i].rearrange("p (s u) -> p s u", u=2),
+                planes[:].rearrange("p (u s) -> p s u", u=2)[:, s0:s1],
             )
 
         def quantise(i, s0, s1):
             nc.vector.quantize_mx(
                 out=codes[i][:, s0:s1].bitcast(FP8X4),
                 scales=scales[i][:, s0:s1],
-                in_=picked[i][:, s0:s1].rearrange("p s j -> p (s j)"),
+                in_=picked[i][:, 2 * s0 : 2 * s1].bitcast(BF16),
             )
 
-        cast(nc.vector.tensor_copy, 0, 0, T)
-        nc.scalar.copy(row_of[:, 0:4:2, 0:T], raw[:, 0:2])
+        SHARE = 256
+        cast(nc.vector.tensor_copy, 0, 0, SHARE)
+        cast(nc.scalar.copy, 0, SHARE, T)
         cast(nc.scalar.copy, 1, 0, T)
-        nc.scalar.copy(row_of[:, 1:4:2, 0:T], raw[:, 2:4])
-        for i in range(2):
-            pick_pairs(i, 0)
-        for j in range(4):
-            pick_row(5, j)
-        for t0, t1 in ((0, 128), (128, 256), (256, T)):
-            nc.gpsimd.tensor_scalar(
-                picked[2][:, t0:t1], raw[:, :, t0:t1].rearrange("p j t -> p t j"), 1.0, 0.0, MULT, ADD
-            )
-        for i in range(2):
-            pick_pairs(i, 1)
-        for i in range(2):
+        pick_pairs(0, 0, S // 2)
+        pick_pairs(0, S // 2, S)
+        nc.scalar.copy(
+            picked[3].rearrange("p (t u) -> p t u", u=2),
+            pairs[:].bitcast(U32).rearrange("p (u t) -> p t u", u=2)[:, 0:T],
+        )
+        for i in range(3):
+            pick_pairs(1, *spans[i])
             interleave(i)
-        for i, s0, s1 in ((0, 0, 256), (0, 256, 512), (0, 512, 640), (1, 0, 128), (2, 0, 256), (2, 256, 384)):
-            quantise(i, s0, s1)
+            quantise(i, 0, 2 * C)
+        codes.append(keep.tile([P, T], U32, name="last_picked", align_bytes=64))
+        quantise(3, 0, 256)
+        quantise(3, 256, T)
 
         y = [keep.tile([P, S], F32, name=f"y{m}") for m in range(M_TILES)]
         ys = [keep.tile([P, T], F32, name=f"ys{m}") for m in range(M_TILES)]
@@ -162,7 +151,7 @@ def tile_moe_shr_lin_silu_kernel(tc, xT, w_words, w_scales, b, gate, offs, pos1,
             return psum.tile([P, 512], F32, name=f"bank{i}")
 
         def product(sums, e, m, s0, s1):
-            i = [j for j in range(3) if spans[j][0] <= s0 < spans[j][1]][0]
+            i = [j for j in range(4) if spans[j][0] <= s0 < spans[j][1]][0]
             s0, s1 = s0 - spans[i][0], s1 - spans[i][0]
             nc.tensor.matmul_mx(
                 out=sums,
@@ -173,21 +162,20 @@ def tile_moe_shr_lin_silu_kernel(tc, xT, w_words, w_scales, b, gate, offs, pos1,
                 **lhsT(e, m),
             )
 
-        def routed(m):
-            for i, experts in enumerate((range(0, 4), range(4, E))):
-                sums = bank(2 * m + i)
-                for e in experts:
-                    product(sums[:, e % 4 * C : (e % 4 + 1) * C], e, m, e * C, (e + 1) * C)
-                for e in experts:
-                    nc.scalar.activation(
-                        y[m][:, e * C : (e + 1) * C],
-                        sums[:, e % 4 * C : (e % 4 + 1) * C],
-                        SILU,
-                        bias=bias[:, m, e : e + 1],
-                    )
+        def routed(m, experts, i):
+            sums = bank(i)
+            for j, e in enumerate(experts):
+                product(sums[:, j * C : (j + 1) * C], e, m, e * C, (e + 1) * C)
+            for j, e in enumerate(experts):
+                nc.scalar.activation(
+                    y[m][:, e * C : (e + 1) * C],
+                    sums[:, j * C : (j + 1) * C],
+                    SILU,
+                    bias=bias[:, m, e : e + 1],
+                )
 
-        def shared(m):
-            sums = bank(m)
+        def shared(m, i):
+            sums = bank(i)
             for t0, t1 in ((0, 256), (256, T)):
                 product(sums[:, t0:t1], E, m, S + t0, S + t1)
             nc.scalar.activation(ys[m][:], sums[:, 0:T], SILU, bias=bias[:, m, E : E + 1])
@@ -201,11 +189,11 @@ def tile_moe_shr_lin_silu_kernel(tc, xT, w_words, w_scales, b, gate, offs, pos1,
             nc.vector.tensor_tensor(to[m][:, t0:t1], a[m][:, t0:t1], b[m][:, t0:t1], ADD)
 
         def store(m, t0=0, t1=T):
-            nc.sync.dma_start(out[m * P : (m + 1) * P, t0:t1], total[m][:, t0:t1])
+            queue = nc.scalar if m < 2 else nc.sync
+            queue.dma_start(out[m * P : (m + 1) * P, t0:t1], total[m][:, t0:t1])
 
-        def turn_and_add(m, i):
+        def turn_and_add(m, i, terms):
             sums = bank(i)
-            terms = (ys, first, second)
             for t0 in range(0, T, P):
                 for j, term in enumerate(terms):
                     nc.tensor.matmul(
@@ -222,30 +210,36 @@ def tile_moe_shr_lin_silu_kernel(tc, xT, w_words, w_scales, b, gate, offs, pos1,
             sums = bank(i)
             for t0 in range(0, T, P):
                 nc.tensor.transpose(sums[:, t0 : t0 + P], part[m][:, t0 : t0 + P], identity[:])
-            nc.scalar.copy(total[m][:], sums[:, 0:T])
-            store(m)
+            return sums[:, 0:T]
 
         def gathers(m):
             gather(first, m, pos1_t, 0)
             gather(second, m, pos2_t, 1)
 
-        routed(0)
-        routed(1)
+        def routed_late(m, i):
+            routed(m, (4, 0, 1), i)
+            routed(m, (5, 2, 3), i + 1)
+
+        for i in range(3):
+            routed(0, (2 * i, 2 * i + 1), i)
+        routed_late(1, 3)
         gathers(0)
-        shared(0)
-        routed(2)
+        shared(0, 5)
+        routed_late(2, 6)
         gathers(1)
-        shared(1)
-        routed(3)
+        shared(1, 0)
+        shared(2, 1)
         gathers(2)
-        shared(2)
-        shared(3)
-        turn_and_add(0, 4)
-        turn_back(0, 5)
-        turn_and_add(1, 6)
-        turn_back(1, 7)
-        turn_and_add(2, 0)
-        turn_back(2, 1)
+        add(part, ys, first, 2)
+        add(total, part, second, 2)
+        store(2)
+        routed_late(3, 2)
+        shared(3, 4)
+        for m in range(2):
+            turn_and_add(m, (6, 2)[m], (ys, first, second))
+        for m in range(2):
+            nc.scalar.copy(total[m][:], turn_back(m, (5, 7)[m]))
+            store(m)
         LATE = 256
         gather(first, 3, pos1_t, 0)
         gather(second, 3, pos2_t, 1, 0, LATE)

@@ -94,8 +94,8 @@ def tile_moe_shr_lin_silu_kernel(tc, xT, w_words, w_scales, b, gate, offs, pos1,
             )
 
         windows = [pairs[:].bitcast(U32)[:, u * WINDOW : (u + 1) * WINDOW] for u in range(2)]
-        spans = ((0, 2 * C), (2 * C, 4 * C), (4 * C, S), (S, S + T))
-        codes = [keep.tile([P, s1 - s0], U32, name=f"codes{s0}", align_bytes=64) for s0, s1 in spans[:3]]
+        spans = ((0, 2 * C), (2 * C, 4 * C), (4 * C, 5 * C), (5 * C, S), (S, S + T))
+        codes = [keep.tile([P, s1 - s0], U32, name=f"codes{s0}", align_bytes=64) for s0, s1 in spans[:4]]
         scales = [keep.tile([P, s1 - s0], U8, name=f"scales{s0}", align_bytes=64) for s0, s1 in spans]
         planes = keep.tile([P, 2 * S], U32, name="planes", align_bytes=64)
         picked = [
@@ -103,10 +103,8 @@ def tile_moe_shr_lin_silu_kernel(tc, xT, w_words, w_scales, b, gate, offs, pos1,
             for s0, s1 in spans
         ]
 
-        def pick_pairs(u, s0, s1):
-            nc.vector.tensor_copy(
-                planes[:, u * S + s0 : u * S + s1], windows[u].indirect(offs_t[:, s0 // 16 : s1 // 16])
-            )
+        def pick_pairs(u, s0, s1, window):
+            nc.vector.tensor_copy(planes[:, u * S + s0 : u * S + s1], window.indirect(offs_t[:, s0 // 16 : s1 // 16]))
 
         def interleave(i):
             s0, s1 = spans[i]
@@ -126,32 +124,40 @@ def tile_moe_shr_lin_silu_kernel(tc, xT, w_words, w_scales, b, gate, offs, pos1,
         cast(nc.vector.tensor_copy, 0, 0, SHARE)
         cast(nc.scalar.copy, 0, SHARE, T)
         cast(nc.scalar.copy, 1, 0, T)
-        pick_pairs(0, 0, S // 2)
-        pick_pairs(0, S // 2, S)
+        pick_pairs(0, 0, 3 * C, windows[0])
+        pick_pairs(0, 3 * C, 5 * C, windows[0])
         nc.scalar.copy(
-            picked[3].rearrange("p (t u) -> p t u", u=2),
+            picked[4].rearrange("p (t u) -> p t u", u=2),
             pairs[:].bitcast(U32).rearrange("p (u t) -> p t u", u=2)[:, 0:T],
         )
-        for i in range(3):
-            pick_pairs(1, *spans[i])
+        for i in range(4):
+            if i == 2:
+                pick_pairs(0, 5 * C, S, pairs[:].bitcast(U32))
+            pick_pairs(1, *spans[i], windows[1])
             interleave(i)
-            quantise(i, 0, 2 * C)
+            quantise(i, 0, spans[i][1] - spans[i][0])
         codes.append(keep.tile([P, T], U32, name="last_picked", align_bytes=64))
-        quantise(3, 0, 256)
-        quantise(3, 256, T)
+        quantise(4, 0, 256)
+        quantise(4, 256, T)
 
         y = [keep.tile([P, S], F32, name=f"y{m}") for m in range(M_TILES)]
-        ys = [keep.tile([P, T], F32, name=f"ys{m}") for m in range(M_TILES)]
-        first = [keep.tile([P, T], F32, name=f"first{m}") for m in range(M_TILES)]
-        second = [keep.tile([P, T], F32, name=f"second{m}") for m in range(M_TILES)]
-        part = [keep.tile([P, T], F32, name=f"part{m}") for m in range(M_TILES)]
-        total = [keep.tile([P, T], F32, name=f"total{m}") for m in range(M_TILES)]
+
+        def by_row_tile(name):
+            early = [keep.tile([P, T], F32, name=f"{name}{m}")[:] for m in range(2)]
+            late = keep.tile([P, 2 * T], F32, name=f"{name}_late")
+            return early + [late[:, 0:T], late[:, T : 2 * T], late[:]]
+
+        ys = by_row_tile("ys")
+        first = by_row_tile("first")
+        second = by_row_tile("second")
+        part = by_row_tile("part")
+        total = by_row_tile("total")
 
         def bank(i):
             return psum.tile([P, 512], F32, name=f"bank{i}")
 
         def product(sums, e, m, s0, s1):
-            i = [j for j in range(4) if spans[j][0] <= s0 < spans[j][1]][0]
+            i = [j for j in range(5) if spans[j][0] <= s0 < spans[j][1]][0]
             s0, s1 = s0 - spans[i][0], s1 - spans[i][0]
             nc.tensor.matmul_mx(
                 out=sums,
@@ -178,7 +184,7 @@ def tile_moe_shr_lin_silu_kernel(tc, xT, w_words, w_scales, b, gate, offs, pos1,
             sums = bank(i)
             for t0, t1 in ((0, 256), (256, T)):
                 product(sums[:, t0:t1], E, m, S + t0, S + t1)
-            nc.scalar.activation(ys[m][:], sums[:, 0:T], SILU, bias=bias[:, m, E : E + 1])
+            nc.scalar.activation(ys[m], sums[:, 0:T], SILU, bias=bias[:, m, E : E + 1])
 
         def gather(to, m, listed, r, t0=0, t1=T):
             nc.vector.tensor_tensor(
@@ -188,13 +194,13 @@ def tile_moe_shr_lin_silu_kernel(tc, xT, w_words, w_scales, b, gate, offs, pos1,
         def add(to, a, b, m, t0=0, t1=T):
             nc.vector.tensor_tensor(to[m][:, t0:t1], a[m][:, t0:t1], b[m][:, t0:t1], ADD)
 
-        def store(m, t0=0, t1=T):
-            queue = nc.scalar if m < 2 else nc.sync
+        def store(m, t0=0, t1=T, queue=nc.sync):
             queue.dma_start(out[m * P : (m + 1) * P, t0:t1], total[m][:, t0:t1])
 
-        def turn_and_add(m, i, terms):
+        def turn_and_add(m, i, width):
             sums = bank(i)
-            for t0 in range(0, T, P):
+            terms = (ys, first, second)
+            for t0 in range(0, width, P):
                 for j, term in enumerate(terms):
                     nc.tensor.matmul(
                         sums[:, t0 : t0 + P],
@@ -204,48 +210,50 @@ def tile_moe_shr_lin_silu_kernel(tc, xT, w_words, w_scales, b, gate, offs, pos1,
                         start=j == 0,
                         stop=j == len(terms) - 1,
                     )
-            nc.scalar.copy(part[m][:], sums[:, 0:T])
+            nc.scalar.copy(part[m][:, 0:width], sums[:, 0:width])
 
-        def turn_back(m, i):
+        def turn_back(m, i, width):
             sums = bank(i)
-            for t0 in range(0, T, P):
+            for t0 in range(0, width, P):
                 nc.tensor.transpose(sums[:, t0 : t0 + P], part[m][:, t0 : t0 + P], identity[:])
-            return sums[:, 0:T]
+            nc.scalar.copy(total[m][:, 0:width], sums[:, 0:width])
+            store(m, 0, width, nc.scalar)
 
         def gathers(m):
             gather(first, m, pos1_t, 0)
             gather(second, m, pos2_t, 1)
 
-        def routed_late(m, i):
-            routed(m, (4, 0, 1), i)
-            routed(m, (5, 2, 3), i + 1)
+        def routed_late(m, i, j):
+            routed(m, (5, 0, 1, 2), i)
+            routed(m, (3, 4), j)
 
-        for i in range(3):
-            routed(0, (2 * i, 2 * i + 1), i)
-        routed_late(1, 3)
+        for i, experts in enumerate(((0, 1), (2, 3), (4,), (5,))):
+            routed(0, experts, i)
+        routed_late(1, 4, 0)
         gathers(0)
-        shared(0, 5)
-        routed_late(2, 6)
+        shared(0, 7)
+        routed_late(2, 5, 2)
         gathers(1)
-        shared(1, 0)
-        shared(2, 1)
+        shared(1, 3)
+        shared(2, 4)
         gathers(2)
-        add(part, ys, first, 2)
-        add(total, part, second, 2)
-        store(2)
-        routed_late(3, 2)
-        shared(3, 4)
-        for m in range(2):
-            turn_and_add(m, (6, 2)[m], (ys, first, second))
-        for m in range(2):
-            nc.scalar.copy(total[m][:], turn_back(m, (5, 7)[m]))
-            store(m)
+        TURNED = 256
+        routed_late(3, 0, 7)
+        shared(3, 6)
+        turn_and_add(0, 5, T)
+        turn_and_add(1, 0, T)
+        turn_back(0, 3, T)
+        turn_and_add(2, 5, TURNED)
+        turn_back(1, 4, T)
+        turn_back(2, 7, TURNED)
         LATE = 256
         gather(first, 3, pos1_t, 0)
         gather(second, 3, pos2_t, 1, 0, LATE)
-        add(part, ys, first, 3)
+        add(part, ys, first, 4, TURNED, 2 * T)
         gather(second, 3, pos2_t, 1, LATE, T)
         add(total, part, second, 3, 0, LATE)
         store(3, 0, LATE)
+        add(total, part, second, 2, TURNED, T)
+        store(2, TURNED, T)
         add(total, part, second, 3, LATE, T)
         store(3, LATE, T)

@@ -126,10 +126,15 @@ def tile_moe_shr_lin_silu_kernel(tc, xT, w_words, w_scales, b, gate, offs, pos1,
         cast(nc.scalar.copy, 1, 0, T)
         pick_pairs(0, 0, 3 * C, windows[0])
         pick_pairs(0, 3 * C, 5 * C, windows[0])
-        nc.scalar.copy(
-            picked[4].rearrange("p (t u) -> p t u", u=2),
-            pairs[:].bitcast(U32).rearrange("p (u t) -> p t u", u=2)[:, 0:T],
-        )
+        for t0 in range(0, T, P):
+            nc.gpsimd.tensor_scalar(
+                picked[4].bitcast(BF16).rearrange("p (t j) -> p t j", j=4)[:, t0 : t0 + P],
+                raw[:, :, t0 : t0 + P].rearrange("p j t -> p t j"),
+                1.0,
+                0.0,
+                MULT,
+                ADD,
+            )
         for i in range(4):
             if i == 2:
                 pick_pairs(0, 5 * C, S, pairs[:].bitcast(U32))
@@ -237,7 +242,7 @@ def tile_moe_shr_lin_silu_kernel(tc, xT, w_words, w_scales, b, gate, offs, pos1,
         shared(1, 3)
         shared(2, 4)
         gathers(2)
-        TURNED = 256
+        TURNED = 128
         routed_late(3, 0, 7)
         shared(3, 6)
         turn_and_add(0, 5, T)

@@ -50,11 +50,10 @@ def tile_moe_shr_lin_silu_kernel(tc, xT, w_words, w_scales, b, gate, offs, pos1,
         nc.sync.dma_start(offs_t[:], offs)
         nc.sync.dma_start(raw[:, 2:4], x_rows[:, 2:4])
 
-        for h in range(2):
-            nc.vector.memset(scales_w[h][:].bitcast(I32), 0)
         nc.gpsimd.memset(dummy[:], 0.0)
         nc.scalar.activation(dummy[:], dummy[:], SILU)
         for u in range(2):
+            nc.gpsimd.memset(scales_w[u][:].bitcast(I32), 0)
             nc.gpsimd.memset(pairs[:, 2 * (u * WINDOW + T) : 2 * (u + 1) * WINDOW], 0.0)
         identity = keep.tile([P, P], F32, name="identity")
         make_identity(nc, identity[:])
@@ -243,6 +242,7 @@ def tile_moe_shr_lin_silu_kernel(tc, xT, w_words, w_scales, b, gate, offs, pos1,
         shared(2, 4)
         gathers(2)
         TURNED = 128
+        add(part, ys, first, 2, TURNED, T)
         routed_late(3, 0, 7)
         shared(3, 6)
         turn_and_add(0, 5, T)
@@ -254,11 +254,12 @@ def tile_moe_shr_lin_silu_kernel(tc, xT, w_words, w_scales, b, gate, offs, pos1,
         LATE = 256
         gather(first, 3, pos1_t, 0)
         gather(second, 3, pos2_t, 1, 0, LATE)
-        add(part, ys, first, 4, TURNED, 2 * T)
+        rest = gates[:, 0, TURNED:T]
+        nc.vector.tensor_tensor(rest, part[2][:, TURNED:T], second[2][:, TURNED:T], ADD)
+        nc.sync.dma_start(out[2 * P : 3 * P, TURNED:T], rest)
+        add(part, ys, first, 3)
         gather(second, 3, pos2_t, 1, LATE, T)
         add(total, part, second, 3, 0, LATE)
         store(3, 0, LATE)
-        add(total, part, second, 2, TURNED, T)
-        store(2, TURNED, T)
         add(total, part, second, 3, LATE, T)
         store(3, LATE, T)

@@ -39,8 +39,8 @@ def tile_moe_shr_lin_silu_kernel(tc, xT, w_words, w_scales, b, gate, offs, pos1,
 
         raw = keep.tile([P, 4, T], F32, name="raw")
         pairs = keep.tile([P, 4 * WINDOW], BF16, name="pairs", align_bytes=64)
-        words = [keep.tile([P, (E + 1) * N], U8, name=f"words{h}", align_bytes=64) for h in range(2)]
-        scales_w = [keep.tile([P, (E + 1) * N // 2], U8, name=f"scales_w{h}", align_bytes=64) for h in range(2)]
+        words = keep.tile([P, (E + 1) * 2 * N], U8, name="words", align_bytes=64)
+        scales_w = keep.tile([P, (E + 1) * N], U8, name="scales_w", align_bytes=64)
         bias = keep.tile([P, M_TILES, E + 1], F32, name="bias")
         dummy = keep.tile([P, 1], F32, name="dummy")
         gates = keep.tile([P, 2, T], F32, name="gates")
@@ -50,10 +50,10 @@ def tile_moe_shr_lin_silu_kernel(tc, xT, w_words, w_scales, b, gate, offs, pos1,
         nc.sync.dma_start(offs_t[:], offs)
         nc.sync.dma_start(raw[:, 2:4], x_rows[:, 2:4])
 
+        nc.gpsimd.memset(scales_w[:].bitcast(I32), 0)
         nc.gpsimd.memset(dummy[:], 0.0)
         nc.scalar.activation(dummy[:], dummy[:], SILU)
         for u in range(2):
-            nc.gpsimd.memset(scales_w[u][:].bitcast(I32), 0)
             nc.gpsimd.memset(pairs[:, 2 * (u * WINDOW + T) : 2 * (u + 1) * WINDOW], 0.0)
         identity = keep.tile([P, P], F32, name="identity")
         make_identity(nc, identity[:])
@@ -61,23 +61,19 @@ def tile_moe_shr_lin_silu_kernel(tc, xT, w_words, w_scales, b, gate, offs, pos1,
         w_scales_i = w_scales.bitcast(I32)
         w_i = w_words.bitcast(I32)
 
-        def load_weights(h):
+        nc.sync.dma_start(
+            words[:].bitcast(I32).rearrange("p (e c) -> p e c", e=E + 1),
+            w_i[:, 0].rearrange("e p c -> p e c"),
+        )
+        for r in range(4):
             nc.sync.dma_start(
-                words[h][:].bitcast(I32).rearrange("p (e c) -> p e c", e=E + 1),
-                w_i[:, 0, :, h * N // 4 : (h + 1) * N // 4].rearrange("e p c -> p e c"),
+                scales_w[:].bitcast(I32).rearrange("p (e c) -> p e c", e=E + 1)[r:P:32],
+                w_scales_i[:, 0, r:16:4, :].rearrange("e q c -> q e c"),
             )
-            for q in range(4):
-                nc.sync.dma_start(
-                    scales_w[h][:].bitcast(I32).rearrange("p (e c) -> p e c", e=E + 1)[32 * q : 32 * q + 4],
-                    w_scales_i[:, 0, 4 * q : 4 * q + 4, h * N // 8 : (h + 1) * N // 8].rearrange("e q c -> q e c"),
-                )
-
-        load_weights(0)
         nc.sync.dma_start(bias[:], b.rearrange("(m p) e -> p m e", p=P))
-        nc.sync.dma_start(gates[:], gate[:, 0:P, :].rearrange("r p t -> p r t"))
         nc.sync.dma_start(pos1_t[:], pos1)
         nc.sync.dma_start(pos2_t[:], pos2)
-        load_weights(1)
+        nc.sync.dma_start(gates[:], gate[:, 0:P, :].rearrange("r p t -> p r t"))
 
         def cast(engine_copy, u, t0, t1):
             engine_copy(
@@ -86,10 +82,10 @@ def tile_moe_shr_lin_silu_kernel(tc, xT, w_words, w_scales, b, gate, offs, pos1,
             )
 
         def lhsT(e, m):
-            col = e * N // 2 + m % 2 * P
+            col = e * N + m * P
             return dict(
-                lhsT=words[m // 2][:, 2 * col : 2 * (col + P)].bitcast(FP4X4),
-                lhsT_scale=scales_w[m // 2][:, col : col + P],
+                lhsT=words[:, 2 * col : 2 * (col + P)].bitcast(FP4X4),
+                lhsT_scale=scales_w[:, col : col + P],
             )
 
         windows = [pairs[:].bitcast(U32)[:, u * WINDOW : (u + 1) * WINDOW] for u in range(2)]
@@ -201,27 +197,27 @@ def tile_moe_shr_lin_silu_kernel(tc, xT, w_words, w_scales, b, gate, offs, pos1,
         def store(m, t0=0, t1=T, queue=nc.sync):
             queue.dma_start(out[m * P : (m + 1) * P, t0:t1], total[m][:, t0:t1])
 
-        def turn_and_add(m, i, width):
+        def turn_and_add(m, i, t0, t1):
             sums = bank(i)
             terms = (ys, first, second)
-            for t0 in range(0, width, P):
-                for j, term in enumerate(terms):
+            for j, term in enumerate(terms):
+                for t in range(t0, t1, P):
                     nc.tensor.matmul(
-                        sums[:, t0 : t0 + P],
-                        lhsT=term[m][:, t0 : t0 + P],
+                        sums[:, t - t0 : t - t0 + P],
+                        lhsT=term[m][:, t : t + P],
                         rhs=identity[:],
                         is_transpose=True,
-                        start=j == 0,
-                        stop=j == len(terms) - 1,
+                        start=j == 0 and t == t0,
+                        stop=j == len(terms) - 1 and t + P == t1,
                     )
-            nc.scalar.copy(part[m][:, 0:width], sums[:, 0:width])
+            nc.scalar.copy(part[m][:, t0:t1], sums[:, 0 : t1 - t0])
 
-        def turn_back(m, i, width):
+        def turn_back(m, i, t0, t1, queue):
             sums = bank(i)
-            for t0 in range(0, width, P):
-                nc.tensor.transpose(sums[:, t0 : t0 + P], part[m][:, t0 : t0 + P], identity[:])
-            nc.scalar.copy(total[m][:, 0:width], sums[:, 0:width])
-            store(m, 0, width, nc.scalar)
+            for t in range(t0, t1, P):
+                nc.tensor.transpose(sums[:, t - t0 : t - t0 + P], part[m][:, t : t + P], identity[:])
+            nc.scalar.copy(total[m][:, t0:t1], sums[:, 0 : t1 - t0])
+            store(m, t0, t1, queue)
 
         def gathers(m):
             gather(first, m, pos1_t, 0)
@@ -235,28 +231,25 @@ def tile_moe_shr_lin_silu_kernel(tc, xT, w_words, w_scales, b, gate, offs, pos1,
             routed(0, experts, i)
         routed_late(1, 4, 0)
         gathers(0)
-        shared(0, 7)
-        routed_late(2, 5, 2)
+        shared(0, 5)
+        routed_late(2, 6, 3)
         gathers(1)
-        shared(1, 3)
-        shared(2, 4)
+        shared(1, 1)
+        turn_and_add(0, 7, 0, T)
+        routed_late(3, 2, 4)
         gathers(2)
-        TURNED = 128
-        add(part, ys, first, 2, TURNED, T)
-        routed_late(3, 0, 7)
-        shared(3, 6)
-        turn_and_add(0, 5, T)
-        turn_and_add(1, 0, T)
-        turn_back(0, 3, T)
-        turn_and_add(2, 5, TURNED)
-        turn_back(1, 4, T)
-        turn_back(2, 7, TURNED)
+        shared(2, 0)
+        turn_and_add(1, 5, 0, T)
+        turn_back(0, 6, 0, T, nc.sync)
+        shared(3, 3)
         LATE = 256
+        turn_and_add(2, 1, 0, LATE)
+        turn_and_add(2, 7, LATE, T)
+        turn_back(1, 2, 0, T, nc.scalar)
+        turn_back(2, 4, 0, LATE, nc.scalar)
+        turn_back(2, 0, LATE, T, nc.scalar)
         gather(first, 3, pos1_t, 0)
         gather(second, 3, pos2_t, 1, 0, LATE)
-        rest = gates[:, 0, TURNED:T]
-        nc.vector.tensor_tensor(rest, part[2][:, TURNED:T], second[2][:, TURNED:T], ADD)
-        nc.sync.dma_start(out[2 * P : 3 * P, TURNED:T], rest)
         add(part, ys, first, 3)
         gather(second, 3, pos2_t, 1, LATE, T)
         add(total, part, second, 3, 0, LATE)

@@ -39,9 +39,9 @@ def tile_moe_shr_lin_silu_kernel(tc, xT, w_words, w_scales, b, gate, offs, pos1,
 
         raw = keep.tile([P, 4, T], F32, name="raw")
         pairs = keep.tile([P, 4 * WINDOW], BF16, name="pairs", align_bytes=64)
-        words = keep.tile([P, (E + 1) * 2 * N], U8, name="words", align_bytes=64)
+        words = [keep.tile([P, (E + 1) * N], U8, name=f"words{h}", align_bytes=64) for h in range(2)]
         scales_w = keep.tile([P, (E + 1) * N], U8, name="scales_w", align_bytes=64)
-        bias = keep.tile([P, M_TILES, E + 1], F32, name="bias")
+        bias = keep.tile([P, M_TILES, 8], F32, name="bias")
         dummy = keep.tile([P, 1], F32, name="dummy")
         gates = keep.tile([P, 2, T], F32, name="gates")
 
@@ -61,19 +61,23 @@ def tile_moe_shr_lin_silu_kernel(tc, xT, w_words, w_scales, b, gate, offs, pos1,
         w_scales_i = w_scales.bitcast(I32)
         w_i = w_words.bitcast(I32)
 
-        nc.sync.dma_start(
-            words[:].bitcast(I32).rearrange("p (e c) -> p e c", e=E + 1),
-            w_i[:, 0].rearrange("e p c -> p e c"),
-        )
+        def load_words(h):
+            nc.sync.dma_start(
+                words[h][:].bitcast(I32).rearrange("p (e c) -> p e c", e=E + 1),
+                w_i[:, 0, :, h * N // 4 : (h + 1) * N // 4].rearrange("e p c -> p e c"),
+            )
+
+        load_words(0)
         for r in range(4):
             nc.sync.dma_start(
                 scales_w[:].bitcast(I32).rearrange("p (e c) -> p e c", e=E + 1)[r:P:32],
                 w_scales_i[:, 0, r:16:4, :].rearrange("e q c -> q e c"),
             )
-        nc.sync.dma_start(bias[:], b.rearrange("(m p) e -> p m e", p=P))
+        nc.sync.dma_start(bias[:, :, 0 : E + 1], b.rearrange("(m p) e -> p m e", p=P))
+        nc.sync.dma_start(gates[:], gate[:, 0:P, :].rearrange("r p t -> p r t"))
         nc.sync.dma_start(pos1_t[:], pos1)
         nc.sync.dma_start(pos2_t[:], pos2)
-        nc.sync.dma_start(gates[:], gate[:, 0:P, :].rearrange("r p t -> p r t"))
+        load_words(1)
 
         def cast(engine_copy, u, t0, t1):
             engine_copy(
@@ -83,8 +87,9 @@ def tile_moe_shr_lin_silu_kernel(tc, xT, w_words, w_scales, b, gate, offs, pos1,
 
         def lhsT(e, m):
             col = e * N + m * P
+            half = e * N // 2 + m % 2 * P
             return dict(
-                lhsT=words[:, 2 * col : 2 * (col + P)].bitcast(FP4X4),
+                lhsT=words[m // 2][:, 2 * half : 2 * (half + P)].bitcast(FP4X4),
                 lhsT_scale=scales_w[:, col : col + P],
             )
 
@@ -234,18 +239,18 @@ def tile_moe_shr_lin_silu_kernel(tc, xT, w_words, w_scales, b, gate, offs, pos1,
         shared(0, 5)
         routed_late(2, 6, 3)
         gathers(1)
-        shared(1, 1)
-        turn_and_add(0, 7, 0, T)
+        shared(1, 6)
+        turn_and_add(0, 3, 0, T)
         routed_late(3, 2, 4)
         gathers(2)
         shared(2, 0)
         turn_and_add(1, 5, 0, T)
-        turn_back(0, 6, 0, T, nc.sync)
-        shared(3, 3)
+        turn_back(0, 1, 0, T, nc.scalar)
+        shared(3, 7)
         LATE = 256
-        turn_and_add(2, 1, 0, LATE)
-        turn_and_add(2, 7, LATE, T)
-        turn_back(1, 2, 0, T, nc.scalar)
+        turn_and_add(2, 6, 0, LATE)
+        turn_and_add(2, 2, LATE, T)
+        turn_back(1, 3, 0, T, nc.scalar)
         turn_back(2, 4, 0, LATE, nc.scalar)
         turn_back(2, 0, LATE, T, nc.scalar)
         gather(first, 3, pos1_t, 0)

@@ -74,9 +74,9 @@ def tile_moe_shr_lin_silu_kernel(tc, xT, w_words, w_scales, b, gate, offs, pos1,
                 w_scales_i[:, 0, r:16:4, :].rearrange("e q c -> q e c"),
             )
         nc.sync.dma_start(bias[:, :, 0 : E + 1], b.rearrange("(m p) e -> p m e", p=P))
-        nc.sync.dma_start(gates[:], gate[:, 0:P, :].rearrange("r p t -> p r t"))
         nc.sync.dma_start(pos1_t[:], pos1)
         nc.sync.dma_start(pos2_t[:], pos2)
+        nc.sync.dma_start(gates[:], gate[:, 0:P, :].rearrange("r p t -> p r t"))
         load_words(1)
 
         def cast(engine_copy, u, t0, t1):
@@ -236,25 +236,31 @@ def tile_moe_shr_lin_silu_kernel(tc, xT, w_words, w_scales, b, gate, offs, pos1,
             routed(0, experts, i)
         routed_late(1, 4, 0)
         gathers(0)
-        shared(0, 5)
-        routed_late(2, 6, 3)
+        shared(0, 3)
+        routed(2, (5,), 0)
+        routed(2, (0,), 1)
+        routed(2, (1, 2, 3, 4), 4)
         gathers(1)
-        shared(1, 6)
-        turn_and_add(0, 3, 0, T)
-        routed_late(3, 2, 4)
+        shared(1, 0)
+        routed(3, (5, 0, 1, 2), 3)
+        turn_and_add(0, 1, 0, T)
+        routed(3, (3, 4), 4)
         gathers(2)
         shared(2, 0)
         turn_and_add(1, 5, 0, T)
-        turn_back(0, 1, 0, T, nc.scalar)
-        shared(3, 7)
-        LATE = 256
-        turn_and_add(2, 6, 0, LATE)
-        turn_and_add(2, 2, LATE, T)
+        turn_back(0, 2, 0, T, nc.scalar)
+        shared(3, 4)
+        TURNED = 128
+        turn_and_add(2, 6, 0, TURNED)
         turn_back(1, 3, 0, T, nc.scalar)
-        turn_back(2, 4, 0, LATE, nc.scalar)
-        turn_back(2, 0, LATE, T, nc.scalar)
+        turn_back(2, 2, 0, TURNED, nc.scalar)
+        LATE = 256
+        add(part, ys, first, 2, TURNED, T)
         gather(first, 3, pos1_t, 0)
         gather(second, 3, pos2_t, 1, 0, LATE)
+        rest = gates[:, 0, TURNED:T]
+        nc.vector.tensor_tensor(rest, part[2][:, TURNED:T], second[2][:, TURNED:T], ADD)
+        nc.sync.dma_start(out[2 * P : 3 * P, TURNED:T], rest)
         add(part, ys, first, 3)
         gather(second, 3, pos2_t, 1, LATE, T)
         add(total, part, second, 3, 0, LATE)

@@ -234,36 +234,35 @@ def tile_moe_shr_lin_silu_kernel(tc, xT, w_words, w_scales, b, gate, offs, pos1,
 
         for i, experts in enumerate(((0, 1), (2, 3), (4,), (5,))):
             routed(0, experts, i)
-        routed_late(1, 4, 0)
+        routed_late(1, 4, 2)
         gathers(0)
         shared(0, 3)
         routed(2, (5,), 0)
-        routed(2, (0,), 1)
+        routed(2, (0,), 2)
         routed(2, (1, 2, 3, 4), 4)
         gathers(1)
         shared(1, 0)
         routed(3, (5, 0, 1, 2), 3)
-        turn_and_add(0, 1, 0, T)
+        turn_and_add(0, 2, 0, T)
         routed(3, (3, 4), 4)
         gathers(2)
         shared(2, 0)
-        turn_and_add(1, 5, 0, T)
-        turn_back(0, 2, 0, T, nc.scalar)
         shared(3, 4)
-        TURNED = 128
-        turn_and_add(2, 6, 0, TURNED)
-        turn_back(1, 3, 0, T, nc.scalar)
-        turn_back(2, 2, 0, TURNED, nc.scalar)
+        turn_and_add(1, 5, 0, T)
+        turn_back(0, 1, 0, T, nc.sync)
         LATE = 256
-        add(part, ys, first, 2, TURNED, T)
+        turn_and_add(2, 6, 0, LATE)
+        turn_back(1, 3, 0, T, nc.scalar)
+        turn_back(2, 7, 0, LATE, nc.scalar)
         gather(first, 3, pos1_t, 0)
-        gather(second, 3, pos2_t, 1, 0, LATE)
-        rest = gates[:, 0, TURNED:T]
-        nc.vector.tensor_tensor(rest, part[2][:, TURNED:T], second[2][:, TURNED:T], ADD)
-        nc.sync.dma_start(out[2 * P : 3 * P, TURNED:T], rest)
-        add(part, ys, first, 3)
         gather(second, 3, pos2_t, 1, LATE, T)
+        add(part, ys, first, 4, LATE, 2 * T)
+        gather(second, 3, pos2_t, 1, 0, LATE)
+
+        def ends(tiles):
+            return tiles[4].rearrange("p (m t) -> p m t", m=2)[:, :, LATE:T]
+
+        nc.vector.tensor_tensor(ends(total), ends(part), ends(second), ADD)
+        nc.sync.dma_start(out[2 * P : 4 * P, LATE:T].rearrange("(m p) t -> p m t", p=P), ends(total))
         add(total, part, second, 3, 0, LATE)
         store(3, 0, LATE)
-        add(total, part, second, 3, LATE, T)
-        store(3, LATE, T)

@@ -5,7 +5,8 @@ from contextlib import ExitStack
 K, T, E, C, N = 512, 384, 6, 128, 512
 S = E * C
 P = 128
-M_TILES = N // P
+ROW_TILES = N // P
+SHARED = E
 
 F32 = mybir.dt.float32
 BF16 = mybir.dt.bfloat16
@@ -24,6 +25,11 @@ FLOPS = 2 * K * N * (S + T)
 BYTES = 4 * K * T + (E + 1) * (K * N // 2 + K * N // 32) + 4 * N * (E + 1) + 2 * 4 * T + 2 * 128 * (48 + 24 + 24) + 4 * N * T
 
 WINDOW = 512
+BANK = 512
+LISTED = 16
+VECTOR_CAST = 256
+WIDE = 256
+TURNED = 256
 
 
 def tile_moe_shr_lin_silu_kernel(tc, xT, w_words, w_scales, b, gate, offs, pos1, pos2, out):
@@ -33,16 +39,16 @@ def tile_moe_shr_lin_silu_kernel(tc, xT, w_words, w_scales, b, gate, offs, pos1,
         keep = ctx.enter_context(tc.tile_pool(name="keep", bufs=1))
         psum = ctx.enter_context(tc.psum_pool(name="psum", bufs=1))
 
-        offs_t = lists.tile([P, S // 16], U16, name="offs_t")
-        pos1_t = lists.tile([P, T // 16], U16, name="pos1_t")
-        pos2_t = lists.tile([P, T // 16], U16, name="pos2_t")
+        offs_t = lists.tile([P, S // LISTED], U16, name="offs_t")
+        pos1_t = lists.tile([P, T // LISTED], U16, name="pos1_t")
+        pos2_t = lists.tile([P, T // LISTED], U16, name="pos2_t")
 
         raw = keep.tile([P, 4, T], F32, name="raw")
         pairs = keep.tile([P, 4 * WINDOW], BF16, name="pairs", align_bytes=64)
         words = [keep.tile([P, (E + 1) * N], U8, name=f"words{h}", align_bytes=64) for h in range(2)]
         scales_w = keep.tile([P, (E + 1) * N], U8, name="scales_w", align_bytes=64)
-        bias = keep.tile([P, M_TILES, 8], F32, name="bias")
-        dummy = keep.tile([P, 1], F32, name="dummy")
+        bias = keep.tile([P, ROW_TILES, 8], F32, name="bias")
+        table_load = keep.tile([P, 1], F32, name="table_load")
         gates = keep.tile([P, 2, T], F32, name="gates")
 
         x_rows = xT.rearrange("(p j) t -> p j t", j=4)
@@ -51,20 +57,20 @@ def tile_moe_shr_lin_silu_kernel(tc, xT, w_words, w_scales, b, gate, offs, pos1,
         nc.sync.dma_start(raw[:, 2:4], x_rows[:, 2:4])
 
         nc.gpsimd.memset(scales_w[:].bitcast(I32), 0)
-        nc.gpsimd.memset(dummy[:], 0.0)
-        nc.scalar.activation(dummy[:], dummy[:], SILU)
+        nc.gpsimd.memset(table_load[:], 0.0)
+        nc.scalar.activation(table_load[:], table_load[:], SILU)
         for u in range(2):
             nc.gpsimd.memset(pairs[:, 2 * (u * WINDOW + T) : 2 * (u + 1) * WINDOW], 0.0)
         identity = keep.tile([P, P], F32, name="identity")
         make_identity(nc, identity[:])
 
         w_scales_i = w_scales.bitcast(I32)
-        w_i = w_words.bitcast(I32)
+        w_words_i = w_words.bitcast(I32)
 
         def load_words(h):
             nc.sync.dma_start(
                 words[h][:].bitcast(I32).rearrange("p (e c) -> p e c", e=E + 1),
-                w_i[:, 0, :, h * N // 4 : (h + 1) * N // 4].rearrange("e p c -> p e c"),
+                w_words_i[:, 0, :, h * N // 4 : (h + 1) * N // 4].rearrange("e p c -> p e c"),
             )
 
         load_words(0)
@@ -85,73 +91,77 @@ def tile_moe_shr_lin_silu_kernel(tc, xT, w_words, w_scales, b, gate, offs, pos1,
                 raw[:, 2 * u : 2 * u + 2, t0:t1].rearrange("p e t -> p t e"),
             )
 
-        def lhsT(e, m):
-            col = e * N + m * P
-            half = e * N // 2 + m % 2 * P
+        def weights(e, m):
+            word = e * N // 2 + m % 2 * P
+            scale = e * N + m * P
             return dict(
-                lhsT=words[m // 2][:, 2 * half : 2 * (half + P)].bitcast(FP4X4),
-                lhsT_scale=scales_w[:, col : col + P],
+                lhsT=words[m // 2][:, 2 * word : 2 * (word + P)].bitcast(FP4X4),
+                lhsT_scale=scales_w[:, scale : scale + P],
             )
 
         windows = [pairs[:].bitcast(U32)[:, u * WINDOW : (u + 1) * WINDOW] for u in range(2)]
-        spans = ((0, 2 * C), (2 * C, 4 * C), (4 * C, 5 * C), (5 * C, S), (S, S + T))
-        codes = [keep.tile([P, s1 - s0], U32, name=f"codes{s0}", align_bytes=64) for s0, s1 in spans[:4]]
-        scales = [keep.tile([P, s1 - s0], U8, name=f"scales{s0}", align_bytes=64) for s0, s1 in spans]
-        planes = keep.tile([P, 2 * S], U32, name="planes", align_bytes=64)
-        picked = [
-            keep.tile([P, 2 * (s1 - s0)], U32, name="last_picked" if s1 == S else f"picked{s0}", align_bytes=64)[:]
-            for s0, s1 in spans
+        chunks = ((0, 2 * C), (2 * C, 4 * C), (4 * C, 5 * C), (5 * C, S), (S, S + T))
+        slot_chunks = len(chunks) - 1
+        codes = [keep.tile([P, s1 - s0], U32, name=f"codes{s0}", align_bytes=64) for s0, s1 in chunks[:slot_chunks]]
+        scales = [keep.tile([P, s1 - s0], U8, name=f"scales{s0}", align_bytes=64) for s0, s1 in chunks]
+        picked = keep.tile([P, 2 * S], U32, name="picked", align_bytes=64)
+        grouped = [
+            keep.tile([P, 2 * (s1 - s0)], U32, name="last_grouped" if s1 == S else f"grouped{s0}", align_bytes=64)[:]
+            for s0, s1 in chunks
         ]
 
         def pick_pairs(u, s0, s1, window):
-            nc.vector.tensor_copy(planes[:, u * S + s0 : u * S + s1], window.indirect(offs_t[:, s0 // 16 : s1 // 16]))
+            nc.vector.tensor_copy(
+                picked[:, u * S + s0 : u * S + s1], window.indirect(offs_t[:, s0 // LISTED : s1 // LISTED])
+            )
 
         def interleave(i):
-            s0, s1 = spans[i]
+            s0, s1 = chunks[i]
             nc.scalar.copy(
-                picked[i].rearrange("p (s u) -> p s u", u=2),
-                planes[:].rearrange("p (u s) -> p s u", u=2)[:, s0:s1],
+                grouped[i].rearrange("p (s u) -> p s u", u=2),
+                picked[:].rearrange("p (u s) -> p s u", u=2)[:, s0:s1],
             )
 
-        def quantise(i, s0, s1):
+        def quantise(i, c0, c1):
             nc.vector.quantize_mx(
-                out=codes[i][:, s0:s1].bitcast(FP8X4),
-                scales=scales[i][:, s0:s1],
-                in_=picked[i][:, 2 * s0 : 2 * s1].bitcast(BF16),
+                out=codes[i][:, c0:c1].bitcast(FP8X4),
+                scales=scales[i][:, c0:c1],
+                in_=grouped[i][:, 2 * c0 : 2 * c1].bitcast(BF16),
             )
 
-        SHARE = 256
-        cast(nc.vector.tensor_copy, 0, 0, SHARE)
-        cast(nc.scalar.copy, 0, SHARE, T)
+        cast(nc.vector.tensor_copy, 0, 0, VECTOR_CAST)
+        cast(nc.scalar.copy, 0, VECTOR_CAST, T)
         cast(nc.scalar.copy, 1, 0, T)
         pick_pairs(0, 0, 3 * C, windows[0])
         pick_pairs(0, 3 * C, 5 * C, windows[0])
         for t0 in range(0, T, P):
             nc.gpsimd.tensor_scalar(
-                picked[4].bitcast(BF16).rearrange("p (t j) -> p t j", j=4)[:, t0 : t0 + P],
+                grouped[slot_chunks].bitcast(BF16).rearrange("p (t j) -> p t j", j=4)[:, t0 : t0 + P],
                 raw[:, :, t0 : t0 + P].rearrange("p j t -> p t j"),
                 1.0,
                 0.0,
                 MULT,
                 ADD,
             )
-        for i in range(4):
-            if i == 2:
+        for i in range(slot_chunks):
+            if chunks[i][0] == 4 * C:
                 pick_pairs(0, 5 * C, S, pairs[:].bitcast(U32))
-            pick_pairs(1, *spans[i], windows[1])
+            pick_pairs(1, *chunks[i], windows[1])
             interleave(i)
-            quantise(i, 0, spans[i][1] - spans[i][0])
-        codes.append(keep.tile([P, T], U32, name="last_picked", align_bytes=64))
-        quantise(4, 0, 256)
-        quantise(4, 256, T)
+            for c0 in range(0, chunks[i][1] - chunks[i][0], C):
+                quantise(i, c0, c0 + C)
+        codes.append(keep.tile([P, T], U32, name="last_grouped", align_bytes=64))
+        quantise(slot_chunks, 0, WIDE)
+        quantise(slot_chunks, WIDE, T)
 
-        y = [keep.tile([P, S], F32, name=f"y{m}") for m in range(M_TILES)]
+        y = [keep.tile([P, S], F32, name=f"y{m}") for m in range(ROW_TILES)]
 
         def by_row_tile(name):
             early = [keep.tile([P, T], F32, name=f"{name}{m}")[:] for m in range(2)]
             late = keep.tile([P, 2 * T], F32, name=f"{name}_late")
             return early + [late[:, 0:T], late[:, T : 2 * T], late[:]]
 
+        both_late = ROW_TILES
         ys = by_row_tile("ys")
         first = by_row_tile("first")
         second = by_row_tile("second")
@@ -159,18 +169,18 @@ def tile_moe_shr_lin_silu_kernel(tc, xT, w_words, w_scales, b, gate, offs, pos1,
         total = by_row_tile("total")
 
         def bank(i):
-            return psum.tile([P, 512], F32, name=f"bank{i}")
+            return psum.tile([P, BANK], F32, name=f"bank{i}")
 
         def product(sums, e, m, s0, s1):
-            i = [j for j in range(5) if spans[j][0] <= s0 < spans[j][1]][0]
-            s0, s1 = s0 - spans[i][0], s1 - spans[i][0]
+            i = [j for j in range(len(chunks)) if chunks[j][0] <= s0 < chunks[j][1]][0]
+            c0, c1 = s0 - chunks[i][0], s1 - chunks[i][0]
             nc.tensor.matmul_mx(
                 out=sums,
-                rhs=codes[i][:, s0:s1].bitcast(FP8X4),
-                rhs_scale=scales[i][:, s0:s1],
+                rhs=codes[i][:, c0:c1].bitcast(FP8X4),
+                rhs_scale=scales[i][:, c0:c1],
                 start=True,
                 stop=True,
-                **lhsT(e, m),
+                **weights(e, m),
             )
 
         def routed(m, experts, i):
@@ -187,82 +197,74 @@ def tile_moe_shr_lin_silu_kernel(tc, xT, w_words, w_scales, b, gate, offs, pos1,
 
         def shared(m, i):
             sums = bank(i)
-            for t0, t1 in ((0, 256), (256, T)):
-                product(sums[:, t0:t1], E, m, S + t0, S + t1)
-            nc.scalar.activation(ys[m], sums[:, 0:T], SILU, bias=bias[:, m, E : E + 1])
+            for t0, t1 in ((0, WIDE), (WIDE, T)):
+                product(sums[:, t0:t1], SHARED, m, S + t0, S + t1)
+            nc.scalar.activation(ys[m], sums[:, 0:T], SILU, bias=bias[:, m, SHARED : SHARED + 1])
 
         def gather(to, m, listed, r, t0=0, t1=T):
             nc.vector.tensor_tensor(
-                to[m][:, t0:t1], y[m][:].indirect(listed[:, t0 // 16 : t1 // 16]), gates[:, r, t0:t1], MULT
+                to[m][:, t0:t1], y[m][:].indirect(listed[:, t0 // LISTED : t1 // LISTED]), gates[:, r, t0:t1], MULT
             )
-
-        def add(to, a, b, m, t0=0, t1=T):
-            nc.vector.tensor_tensor(to[m][:, t0:t1], a[m][:, t0:t1], b[m][:, t0:t1], ADD)
-
-        def store(m, t0=0, t1=T, queue=nc.sync):
-            queue.dma_start(out[m * P : (m + 1) * P, t0:t1], total[m][:, t0:t1])
-
-        def turn_and_add(m, i, t0, t1):
-            sums = bank(i)
-            terms = (ys, first, second)
-            for j, term in enumerate(terms):
-                for t in range(t0, t1, P):
-                    nc.tensor.matmul(
-                        sums[:, t - t0 : t - t0 + P],
-                        lhsT=term[m][:, t : t + P],
-                        rhs=identity[:],
-                        is_transpose=True,
-                        start=j == 0 and t == t0,
-                        stop=j == len(terms) - 1 and t + P == t1,
-                    )
-            nc.scalar.copy(part[m][:, t0:t1], sums[:, 0 : t1 - t0])
-
-        def turn_back(m, i, t0, t1, queue):
-            sums = bank(i)
-            for t in range(t0, t1, P):
-                nc.tensor.transpose(sums[:, t - t0 : t - t0 + P], part[m][:, t : t + P], identity[:])
-            nc.scalar.copy(total[m][:, t0:t1], sums[:, 0 : t1 - t0])
-            store(m, t0, t1, queue)
 
         def gathers(m):
             gather(first, m, pos1_t, 0)
             gather(second, m, pos2_t, 1)
 
-        def routed_late(m, i, j):
-            routed(m, (5, 0, 1, 2), i)
-            routed(m, (3, 4), j)
+        def turn_and_add(m, i, width):
+            sums = bank(i)
+            terms = (ys, first, second)
+            for j, term in enumerate(terms):
+                for t0 in range(0, width, P):
+                    nc.tensor.matmul(
+                        sums[:, t0 : t0 + P],
+                        lhsT=term[m][:, t0 : t0 + P],
+                        rhs=identity[:],
+                        is_transpose=True,
+                        start=j == 0 and t0 == 0,
+                        stop=j == len(terms) - 1 and t0 + P == width,
+                    )
+            nc.scalar.copy(part[m][:, 0:width], sums[:, 0:width])
 
-        for i, experts in enumerate(((0, 1), (2, 3), (4,), (5,))):
-            routed(0, experts, i)
-        routed_late(1, 4, 2)
+        def turn_back(m, i, width, queue):
+            sums = bank(i)
+            for t0 in range(0, width, P):
+                nc.tensor.transpose(sums[:, t0 : t0 + P], part[m][:, t0 : t0 + P], identity[:])
+            nc.scalar.copy(total[m][:, 0:width], sums[:, 0:width])
+            queue.dma_start(out[m * P : (m + 1) * P, 0:width], total[m][:, 0:width])
+
+        for e, i in enumerate((0, 1, 2, 3, 5, 6)):
+            routed(0, (e,), i)
+        routed(1, (5, 0, 1, 2), 4)
+        routed(1, (3, 4), 5)
         gathers(0)
-        shared(0, 3)
+        shared(0, 6)
         routed(2, (5,), 0)
-        routed(2, (0,), 2)
+        routed(2, (0,), 5)
         routed(2, (1, 2, 3, 4), 4)
         gathers(1)
         shared(1, 0)
-        routed(3, (5, 0, 1, 2), 3)
-        turn_and_add(0, 2, 0, T)
+        routed(3, (5, 0, 1, 2), 6)
+        turn_and_add(0, 5, T)
         routed(3, (3, 4), 4)
         gathers(2)
         shared(2, 0)
         shared(3, 4)
-        turn_and_add(1, 5, 0, T)
-        turn_back(0, 1, 0, T, nc.sync)
-        LATE = 256
-        turn_and_add(2, 6, 0, LATE)
-        turn_back(1, 3, 0, T, nc.scalar)
-        turn_back(2, 7, 0, LATE, nc.scalar)
+        turn_and_add(1, 2, T)
+        turn_back(0, 1, T, nc.sync)
+        turn_and_add(2, 3, TURNED)
+        turn_back(1, 6, T, nc.scalar)
+        turn_back(2, 7, TURNED, nc.scalar)
+
+        def ends(views):
+            return views[both_late].rearrange("p (m t) -> p m t", m=2)[:, :, TURNED:T]
+
         gather(first, 3, pos1_t, 0)
-        gather(second, 3, pos2_t, 1, LATE, T)
-        add(part, ys, first, 4, LATE, 2 * T)
-        gather(second, 3, pos2_t, 1, 0, LATE)
-
-        def ends(tiles):
-            return tiles[4].rearrange("p (m t) -> p m t", m=2)[:, :, LATE:T]
-
+        gather(second, 3, pos2_t, 1, TURNED, T)
+        nc.vector.tensor_tensor(
+            part[both_late][:, TURNED : 2 * T], ys[both_late][:, TURNED : 2 * T], first[both_late][:, TURNED : 2 * T], ADD
+        )
+        gather(second, 3, pos2_t, 1, 0, TURNED)
         nc.vector.tensor_tensor(ends(total), ends(part), ends(second), ADD)
-        nc.sync.dma_start(out[2 * P : 4 * P, LATE:T].rearrange("(m p) t -> p m t", p=P), ends(total))
-        add(total, part, second, 3, 0, LATE)
-        store(3, 0, LATE)
+        nc.sync.dma_start(out[2 * P : 4 * P, TURNED:T].rearrange("(m p) t -> p m t", p=P), ends(total))
+        nc.vector.tensor_tensor(total[3][:, 0:TURNED], part[3][:, 0:TURNED], second[3][:, 0:TURNED], ADD)
+        nc.sync.dma_start(out[3 * P : 4 * P, 0:TURNED], total[3][:, 0:TURNED])

@@ -1,10 +1,10 @@
 import concourse.mybir as mybir
-from concourse.masks import make_identity
 from contextlib import ExitStack
 
 K, T, E, C, N = 512, 384, 6, 128, 512
 S = E * C
 P = 128
+QUAD = 32
 ROW_TILES = N // P
 SHARED = E
 
@@ -19,12 +19,16 @@ FP4X4 = mybir.dt.float4_e2m1fn_x4
 
 MULT = mybir.AluOpType.mult
 ADD = mybir.AluOpType.add
+EQUAL = mybir.AluOpType.is_equal
 SILU = mybir.ActivationFunctionType.Silu
+COPY = mybir.ActivationFunctionType.Copy
 
 FLOPS = 2 * K * N * (S + T)
 BYTES = 4 * K * T + (E + 1) * (K * N // 2 + K * N // 32) + 4 * N * (E + 1) + 2 * 4 * T + 2 * 128 * (48 + 24 + 24) + 4 * N * T
 
 WINDOW = 512
+LONG_WINDOW = 896
+SCALAR_CAST = 256
 BANK = 512
 LISTED = 16
 VECTOR_CAST = 256
@@ -43,8 +47,10 @@ def tile_moe_shr_lin_silu_kernel(tc, xT, w_words, w_scales, b, gate, offs, pos1,
         pos1_t = lists.tile([P, T // LISTED], U16, name="pos1_t")
         pos2_t = lists.tile([P, T // LISTED], U16, name="pos2_t")
 
-        raw = keep.tile([P, 4, T], F32, name="raw")
-        pairs = keep.tile([P, 4 * WINDOW], BF16, name="pairs", align_bytes=64)
+        tokens = keep.tile([P, 7 * T], U32, name="tokens", align_bytes=64)
+        table_at = (2 * T, T)
+        rows = tokens[:].bitcast(BF16)
+        raw = tokens[:, 3 * T : 7 * T].bitcast(F32).rearrange("p (j t) -> p j t", j=4)
         words = [keep.tile([P, (E + 1) * N], U8, name=f"words{h}", align_bytes=64) for h in range(2)]
         scales_w = keep.tile([P, (E + 1) * N], U8, name="scales_w", align_bytes=64)
         bias = keep.tile([P, ROW_TILES, 8], F32, name="bias")
@@ -59,10 +65,15 @@ def tile_moe_shr_lin_silu_kernel(tc, xT, w_words, w_scales, b, gate, offs, pos1,
         nc.gpsimd.memset(scales_w[:].bitcast(I32), 0)
         nc.gpsimd.memset(table_load[:], 0.0)
         nc.scalar.activation(table_load[:], table_load[:], SILU)
-        for u in range(2):
-            nc.gpsimd.memset(pairs[:, 2 * (u * WINDOW + T) : 2 * (u + 1) * WINDOW], 0.0)
         identity = keep.tile([P, P], F32, name="identity")
-        make_identity(nc, identity[:])
+        ones, count, lane = (keep.tile([P, QUAD], F32, name=name, align_bytes=64) for name in ("ones", "count", "lane"))
+        nc.vector.memset(ones[:], 1.0)
+        nc.vector.memset(identity[:], 0.0)
+        nc.vector.tensor_tensor_scan(count[:], ones[:], ones[:], 0.0, MULT, ADD)
+        nc.vector.transpose(lane[:], count[:])
+        for q0 in range(0, P, QUAD):
+            block = slice(q0, q0 + QUAD)
+            nc.vector.tensor_tensor(identity[block, block], count[block], lane[block], EQUAL)
 
         w_scales_i = w_scales.bitcast(I32)
         w_words_i = w_words.bitcast(I32)
@@ -87,9 +98,12 @@ def tile_moe_shr_lin_silu_kernel(tc, xT, w_words, w_scales, b, gate, offs, pos1,
 
         def cast(engine_copy, u, t0, t1):
             engine_copy(
-                pairs[:, 2 * (u * WINDOW + t0) : 2 * (u * WINDOW + t1)].rearrange("p (t e) -> p t e", e=2),
+                tokens[:, table_at[u] + t0 : table_at[u] + t1].bitcast(BF16).rearrange("p (t e) -> p t e", e=2),
                 raw[:, 2 * u : 2 * u + 2, t0:t1].rearrange("p e t -> p t e"),
             )
+
+        def round_on_gpsimd(to, values):
+            nc.gpsimd.tensor_scalar(to, values, 1.0, 0.0, MULT, ADD)
 
         def weights(e, m):
             word = e * N // 2 + m % 2 * P
@@ -99,28 +113,21 @@ def tile_moe_shr_lin_silu_kernel(tc, xT, w_words, w_scales, b, gate, offs, pos1,
                 lhsT_scale=scales_w[:, scale : scale + P],
             )
 
-        windows = [pairs[:].bitcast(U32)[:, u * WINDOW : (u + 1) * WINDOW] for u in range(2)]
-        chunks = ((0, 2 * C), (2 * C, 4 * C), (4 * C, 5 * C), (5 * C, S), (S, S + T))
-        slot_chunks = len(chunks) - 1
+        chunks = ((0, 2 * C), (2 * C, 4 * C), (4 * C, 5 * C), (5 * C, S), (S, S + WIDE), (S + WIDE, S + T))
+        slot_chunks = len(chunks) - 2
         codes = [keep.tile([P, s1 - s0], U32, name=f"codes{s0}", align_bytes=64) for s0, s1 in chunks[:slot_chunks]]
         scales = [keep.tile([P, s1 - s0], U8, name=f"scales{s0}", align_bytes=64) for s0, s1 in chunks]
-        picked = keep.tile([P, 2 * S], U32, name="picked", align_bytes=64)
         grouped = [
             keep.tile([P, 2 * (s1 - s0)], U32, name="last_grouped" if s1 == S else f"grouped{s0}", align_bytes=64)[:]
-            for s0, s1 in chunks
+            for s0, s1 in chunks[:-1]
         ]
 
-        def pick_pairs(u, s0, s1, window):
-            nc.vector.tensor_copy(
-                picked[:, u * S + s0 : u * S + s1], window.indirect(offs_t[:, s0 // LISTED : s1 // LISTED])
-            )
+        def pick_pairs(to, u, s0, s1, width):
+            window = tokens[:, table_at[u] : table_at[u] + width]
+            nc.vector.tensor_copy(to, window.indirect(offs_t[:, s0 // LISTED : s1 // LISTED]))
 
-        def interleave(i):
-            s0, s1 = chunks[i]
-            nc.scalar.copy(
-                grouped[i].rearrange("p (s u) -> p s u", u=2),
-                picked[:].rearrange("p (u s) -> p s u", u=2)[:, s0:s1],
-            )
+        def interleave(i, planes):
+            nc.scalar.copy(grouped[i].rearrange("p (s u) -> p s u", u=2), planes.rearrange("p u s -> p s u"))
 
         def quantise(i, c0, c1):
             nc.vector.quantize_mx(
@@ -131,28 +138,38 @@ def tile_moe_shr_lin_silu_kernel(tc, xT, w_words, w_scales, b, gate, offs, pos1,
 
         cast(nc.vector.tensor_copy, 0, 0, VECTOR_CAST)
         cast(nc.scalar.copy, 0, VECTOR_CAST, T)
-        cast(nc.scalar.copy, 1, 0, T)
-        pick_pairs(0, 0, 3 * C, windows[0])
-        pick_pairs(0, 3 * C, 5 * C, windows[0])
-        for t0 in range(0, T, P):
-            nc.gpsimd.tensor_scalar(
+        nc.scalar.copy(rows[:, 0:T], raw[:, 0])
+        round_on_gpsimd(rows[:, T : 2 * T], rows[:, 2 * table_at[0] + 1 : 2 * (table_at[0] + T) : 2])
+        cast(nc.scalar.copy, 1, 0, SCALAR_CAST)
+        cast(round_on_gpsimd, 1, SCALAR_CAST, T)
+        picked_tile = keep.tile([P, 2 * S], U32, name="picked", align_bytes=64)
+        picked = picked_tile[:].rearrange("p (u s) -> p u s", u=2)
+        pick_pairs(picked[:, 0, 0 : 5 * C], 0, 0, 5 * C, LONG_WINDOW)
+        for e in range(2):
+            nc.scalar.activation(
+                picked[:, 0, 5 * C : S].bitcast(BF16)[:, e : 2 * C : 2],
+                rows[:, e * T : e * T + WINDOW].indirect(offs_t[:, 5 * C // LISTED : S // LISTED]),
+                COPY,
+            )
+        for t0 in range(0, WIDE, P):
+            round_on_gpsimd(
                 grouped[slot_chunks].bitcast(BF16).rearrange("p (t j) -> p t j", j=4)[:, t0 : t0 + P],
                 raw[:, :, t0 : t0 + P].rearrange("p j t -> p t j"),
-                1.0,
-                0.0,
-                MULT,
-                ADD,
             )
         for i in range(slot_chunks):
-            if chunks[i][0] == 4 * C:
-                pick_pairs(0, 5 * C, S, pairs[:].bitcast(U32))
-            pick_pairs(1, *chunks[i], windows[1])
-            interleave(i)
-            for c0 in range(0, chunks[i][1] - chunks[i][0], C):
+            s0, s1 = chunks[i]
+            pick_pairs(picked[:, 1, s0:s1], 1, s0, s1, WINDOW)
+            interleave(i, picked[:, :, s0:s1])
+            for c0 in range(0, s1 - s0, C):
                 quantise(i, c0, c0 + C)
-        codes.append(keep.tile([P, T], U32, name="last_grouped", align_bytes=64))
+        codes.append(keep.tile([P, WIDE], U32, name="last_grouped", align_bytes=64))
+        codes.append(keep.tile([P, T - WIDE], U32, name="codes_rest", align_bytes=64))
+        grouped.append(keep.tile([P, 2 * (T - WIDE)], U32, name=f"grouped{4 * C}", align_bytes=64)[:])
+        nc.vector.tensor_copy(
+            grouped[-1].bitcast(BF16).rearrange("p (t j) -> p t j", j=4), raw[:, :, WIDE:T].rearrange("p j t -> p t j")
+        )
         quantise(slot_chunks, 0, WIDE)
-        quantise(slot_chunks, WIDE, T)
+        quantise(slot_chunks + 1, 0, T - WIDE)
 
         y = [keep.tile([P, S], F32, name=f"y{m}") for m in range(ROW_TILES)]
 

@@ -218,14 +218,9 @@ def tile_moe_shr_lin_silu_kernel(tc, xT, w_words, w_scales, b, gate, offs, pos1,
                 product(sums[:, t0:t1], SHARED, m, S + t0, S + t1)
             nc.scalar.activation(ys[m], sums[:, 0:T], SILU, bias=bias[:, m, SHARED : SHARED + 1])
 
-        def gather(to, m, listed, r, t0=0, t1=T):
-            nc.vector.tensor_tensor(
-                to[m][:, t0:t1], y[m][:].indirect(listed[:, t0 // LISTED : t1 // LISTED]), gates[:, r, t0:t1], MULT
-            )
-
         def gathers(m):
-            gather(first, m, pos1_t, 0)
-            gather(second, m, pos2_t, 1)
+            nc.vector.tensor_tensor(first[m], y[m][:].indirect(pos1_t[:]), gates[:, 0], MULT)
+            nc.vector.tensor_tensor(second[m], y[m][:].indirect(pos2_t[:]), gates[:, 1], MULT)
 
         def turn_and_add(m, i, width):
             sums = bank(i)
@@ -265,22 +260,19 @@ def tile_moe_shr_lin_silu_kernel(tc, xT, w_words, w_scales, b, gate, offs, pos1,
         routed(3, (3, 4), 4)
         gathers(2)
         shared(2, 0)
-        shared(3, 4)
-        turn_and_add(1, 2, T)
+        shared(3, 6)
         turn_back(0, 1, T, nc.sync)
+        turn_and_add(1, 2, T)
         turn_and_add(2, 3, TURNED)
-        turn_back(1, 6, T, nc.scalar)
+        turn_back(1, 4, T, nc.scalar)
         turn_back(2, 7, TURNED, nc.scalar)
 
         def ends(views):
             return views[both_late].rearrange("p (m t) -> p m t", m=2)[:, :, TURNED:T]
 
-        gather(first, 3, pos1_t, 0)
-        gather(second, 3, pos2_t, 1, TURNED, T)
-        nc.vector.tensor_tensor(
-            part[both_late][:, TURNED : 2 * T], ys[both_late][:, TURNED : 2 * T], first[both_late][:, TURNED : 2 * T], ADD
-        )
-        gather(second, 3, pos2_t, 1, 0, TURNED)
+        gathers(3)
+        nc.vector.tensor_tensor(ends(part), ends(ys), ends(first), ADD)
+        nc.vector.tensor_tensor(part[3][:, 0:TURNED], ys[3][:, 0:TURNED], first[3][:, 0:TURNED], ADD)
         nc.vector.tensor_tensor(ends(total), ends(part), ends(second), ADD)
         nc.sync.dma_start(out[2 * P : 4 * P, TURNED:T].rearrange("(m p) t -> p m t", p=P), ends(total))
         nc.vector.tensor_tensor(total[3][:, 0:TURNED], part[3][:, 0:TURNED], second[3][:, 0:TURNED], ADD)

@@ -127,7 +127,9 @@ def tile_moe_shr_lin_silu_kernel(tc, xT, w_words, w_scales, b, gate, offs, pos1,
             nc.vector.tensor_copy(to, window.indirect(offs_t[:, s0 // LISTED : s1 // LISTED]))
 
         def interleave(i, planes):
-            nc.scalar.copy(grouped[i].rearrange("p (s u) -> p s u", u=2), planes.rearrange("p u s -> p s u"))
+            nc.scalar.copy(
+                grouped[i].bitcast(F32).rearrange("p (s u) -> p s u", u=2), planes.bitcast(F32).rearrange("p u s -> p s u")
+            )
 
         def quantise(i, c0, c1):
             nc.vector.quantize_mx(
@@ -246,24 +248,25 @@ def tile_moe_shr_lin_silu_kernel(tc, xT, w_words, w_scales, b, gate, offs, pos1,
 
         for e, i in enumerate((0, 1, 2, 3, 5, 6)):
             routed(0, (e,), i)
-        routed(1, (5, 0, 1, 2), 4)
+        routed(1, (5, 0), 4)
+        routed(1, (1, 2), 3)
         routed(1, (3, 4), 5)
         gathers(0)
         shared(0, 6)
         routed(2, (5,), 0)
-        routed(2, (0,), 5)
+        routed(2, (0,), 3)
         routed(2, (1, 2, 3, 4), 4)
         gathers(1)
         shared(1, 0)
         routed(3, (5, 0, 1, 2), 6)
-        turn_and_add(0, 5, T)
+        turn_and_add(0, 3, T)
         routed(3, (3, 4), 4)
         gathers(2)
         shared(2, 0)
         shared(3, 6)
         turn_back(0, 1, T, nc.sync)
         turn_and_add(1, 2, T)
-        turn_and_add(2, 3, TURNED)
+        turn_and_add(2, 5, TURNED)
         turn_back(1, 4, T, nc.scalar)
         turn_back(2, 7, TURNED, nc.scalar)
 

@@ -1,10 +1,10 @@
 import concourse.mybir as mybir
+from concourse.masks import make_identity
 from contextlib import ExitStack
 
 K, T, E, C, N = 512, 384, 6, 128, 512
 S = E * C
 P = 128
-QUAD = 32
 ROW_TILES = N // P
 SHARED = E
 
@@ -19,7 +19,6 @@ FP4X4 = mybir.dt.float4_e2m1fn_x4
 
 MULT = mybir.AluOpType.mult
 ADD = mybir.AluOpType.add
-EQUAL = mybir.AluOpType.is_equal
 SILU = mybir.ActivationFunctionType.Silu
 COPY = mybir.ActivationFunctionType.Copy
 
@@ -62,18 +61,11 @@ def tile_moe_shr_lin_silu_kernel(tc, xT, w_words, w_scales, b, gate, offs, pos1,
         nc.sync.dma_start(offs_t[:], offs)
         nc.sync.dma_start(raw[:, 2:4], x_rows[:, 2:4])
 
-        nc.gpsimd.memset(scales_w[:].bitcast(I32), 0)
         nc.gpsimd.memset(table_load[:], 0.0)
         nc.scalar.activation(table_load[:], table_load[:], SILU)
+        nc.gpsimd.memset(scales_w[:].bitcast(I32), 0)
         identity = keep.tile([P, P], F32, name="identity")
-        ones, count, lane = (keep.tile([P, QUAD], F32, name=name, align_bytes=64) for name in ("ones", "count", "lane"))
-        nc.vector.memset(ones[:], 1.0)
-        nc.vector.memset(identity[:], 0.0)
-        nc.vector.tensor_tensor_scan(count[:], ones[:], ones[:], 0.0, MULT, ADD)
-        nc.vector.transpose(lane[:], count[:])
-        for q0 in range(0, P, QUAD):
-            block = slice(q0, q0 + QUAD)
-            nc.vector.tensor_tensor(identity[block, block], count[block], lane[block], EQUAL)
+        make_identity(nc, identity[:])
 
         w_scales_i = w_scales.bitcast(I32)
         w_words_i = w_words.bitcast(I32)

@@ -63,7 +63,7 @@ def tile_moe_shr_lin_silu_kernel(tc, xT, w_words, w_scales, b, gate, offs, pos1,
 
         nc.gpsimd.memset(table_load[:], 0.0)
         nc.scalar.activation(table_load[:], table_load[:], SILU)
-        nc.gpsimd.memset(scales_w[:].bitcast(I32), 0)
+        nc.vector.memset(scales_w[:].bitcast(I32), 0)
         identity = keep.tile([P, P], F32, name="identity")
         make_identity(nc, identity[:])
 

@@ -27,7 +27,7 @@ BYTES = 4 * K * T + (E + 1) * (K * N // 2 + K * N // 32) + 4 * N * (E + 1) + 2 *
 
 WINDOW = 512
 LONG_WINDOW = 896
-SCALAR_CAST = 256
+SCALAR_CAST = 160
 BANK = 512
 LISTED = 16
 VECTOR_CAST = 256
@@ -133,7 +133,10 @@ def tile_moe_shr_lin_silu_kernel(tc, xT, w_words, w_scales, b, gate, offs, pos1,
         cast(nc.vector.tensor_copy, 0, 0, VECTOR_CAST)
         cast(nc.scalar.copy, 0, VECTOR_CAST, T)
         nc.scalar.copy(rows[:, 0:T], raw[:, 0])
-        round_on_gpsimd(rows[:, T : 2 * T], rows[:, 2 * table_at[0] + 1 : 2 * (table_at[0] + T) : 2])
+        nc.scalar.copy(rows[:, T + VECTOR_CAST : 2 * T], raw[:, 1, VECTOR_CAST:T])
+        round_on_gpsimd(
+            rows[:, T : T + VECTOR_CAST], rows[:, 2 * table_at[0] + 1 : 2 * (table_at[0] + VECTOR_CAST) : 2]
+        )
         cast(nc.scalar.copy, 1, 0, SCALAR_CAST)
         cast(round_on_gpsimd, 1, SCALAR_CAST, T)
         picked_tile = keep.tile([P, 2 * S], U32, name="picked", align_bytes=64)

@@ -27,7 +27,8 @@ BYTES = 4 * K * T + (E + 1) * (K * N // 2 + K * N // 32) + 4 * N * (E + 1) + 2 *
 
 WINDOW = 512
 LONG_WINDOW = 896
-SCALAR_CAST = 160
+SCALAR_CAST = 192
+VECTOR_SLOTS = 576
 BANK = 512
 LISTED = 16
 VECTOR_CAST = 256
@@ -105,13 +106,13 @@ def tile_moe_shr_lin_silu_kernel(tc, xT, w_words, w_scales, b, gate, offs, pos1,
                 lhsT_scale=scales_w[:, scale : scale + P],
             )
 
-        chunks = ((0, 2 * C), (2 * C, 4 * C), (4 * C, 5 * C), (5 * C, S), (S, S + WIDE), (S + WIDE, S + T))
+        chunks = ((0, C), (C, 2 * C), (2 * C, 4 * C), (4 * C, 5 * C), (5 * C, S), (S, S + WIDE), (S + WIDE, S + T))
         slot_chunks = len(chunks) - 2
         codes = [keep.tile([P, s1 - s0], U32, name=f"codes{s0}", align_bytes=64) for s0, s1 in chunks[:slot_chunks]]
         scales = [keep.tile([P, s1 - s0], U8, name=f"scales{s0}", align_bytes=64) for s0, s1 in chunks]
         grouped = [
             keep.tile([P, 2 * (s1 - s0)], U32, name="last_grouped" if s1 == S else f"grouped{s0}", align_bytes=64)[:]
-            for s0, s1 in chunks[:-1]
+            for s0, s1 in chunks[:slot_chunks]
         ]
 
         def pick_pairs(to, u, s0, s1, width):
@@ -141,32 +142,36 @@ def tile_moe_shr_lin_silu_kernel(tc, xT, w_words, w_scales, b, gate, offs, pos1,
         cast(round_on_gpsimd, 1, SCALAR_CAST, T)
         picked_tile = keep.tile([P, 2 * S], U32, name="picked", align_bytes=64)
         picked = picked_tile[:].rearrange("p (u s) -> p u s", u=2)
-        pick_pairs(picked[:, 0, 0 : 5 * C], 0, 0, 5 * C, LONG_WINDOW)
+        pick_pairs(picked[:, 0, 0:VECTOR_SLOTS], 0, 0, VECTOR_SLOTS, LONG_WINDOW)
         for e in range(2):
             nc.scalar.activation(
-                picked[:, 0, 5 * C : S].bitcast(BF16)[:, e : 2 * C : 2],
-                rows[:, e * T : e * T + WINDOW].indirect(offs_t[:, 5 * C // LISTED : S // LISTED]),
+                picked[:, 0, VECTOR_SLOTS:S].bitcast(BF16)[:, e : 2 * (S - VECTOR_SLOTS) : 2],
+                rows[:, e * T : e * T + WINDOW].indirect(offs_t[:, VECTOR_SLOTS // LISTED : S // LISTED]),
                 COPY,
-            )
-        for t0 in range(0, WIDE, P):
-            round_on_gpsimd(
-                grouped[slot_chunks].bitcast(BF16).rearrange("p (t j) -> p t j", j=4)[:, t0 : t0 + P],
-                raw[:, :, t0 : t0 + P].rearrange("p j t -> p t j"),
             )
         for i in range(slot_chunks):
             s0, s1 = chunks[i]
-            pick_pairs(picked[:, 1, s0:s1], 1, s0, s1, WINDOW)
-            interleave(i, picked[:, :, s0:s1])
+            if i == 0:
+                pick_pairs(picked[:, 1, 0 : 2 * C], 1, 0, 2 * C, WINDOW)
+                round_on_gpsimd(
+                    grouped[0].bitcast(BF16).rearrange("p (s u e) -> p s u e", u=2, e=2),
+                    picked_tile[:].bitcast(BF16).rearrange("p (u s e) -> p s u e", u=2, e=2)[:, s0:s1],
+                )
+            else:
+                if i > 1:
+                    pick_pairs(picked[:, 1, s0:s1], 1, s0, s1, WINDOW)
+                interleave(i, picked[:, :, s0:s1])
             for c0 in range(0, s1 - s0, C):
                 quantise(i, c0, c0 + C)
-        codes.append(keep.tile([P, WIDE], U32, name="last_grouped", align_bytes=64))
-        codes.append(keep.tile([P, T - WIDE], U32, name="codes_rest", align_bytes=64))
-        grouped.append(keep.tile([P, 2 * (T - WIDE)], U32, name=f"grouped{4 * C}", align_bytes=64)[:])
-        nc.vector.tensor_copy(
-            grouped[-1].bitcast(BF16).rearrange("p (t j) -> p t j", j=4), raw[:, :, WIDE:T].rearrange("p j t -> p t j")
-        )
-        quantise(slot_chunks, 0, WIDE)
+        for (s0, s1), place in zip(chunks[slot_chunks:], ("last_grouped", f"grouped{4 * C}")):
+            grouped.append(keep.tile([P, 2 * (s1 - s0)], U32, name=place, align_bytes=64)[:])
+            codes.append(keep.tile([P, s1 - s0], U32, name=f"codes{s0}", align_bytes=64))
+            nc.vector.tensor_copy(
+                grouped[-1].bitcast(I32).rearrange("p (t u) -> p t u", u=2),
+                tokens[:, T : 3 * T].bitcast(I32).rearrange("p (u t) -> p t u", u=2)[:, s0 - S : s1 - S, ::-1],
+            )
         quantise(slot_chunks + 1, 0, T - WIDE)
+        quantise(slot_chunks, 0, WIDE)
 
         y = [keep.tile([P, S], F32, name=f"y{m}") for m in range(ROW_TILES)]
 

@@ -25,13 +25,14 @@ COPY = mybir.ActivationFunctionType.Copy
 FLOPS = 2 * K * N * (S + T)
 BYTES = 4 * K * T + (E + 1) * (K * N // 2 + K * N // 32) + 4 * N * (E + 1) + 2 * 4 * T + 2 * 128 * (48 + 24 + 24) + 4 * N * T
 
-WINDOW = 512
-LONG_WINDOW = 896
-SCALAR_CAST = 192
-VECTOR_SLOTS = 576
 BANK = 512
 LISTED = 16
+WINDOW = 512
+LONG_WINDOW = 896
 VECTOR_CAST = 256
+SCALAR_CAST = 192
+VECTOR_SLOTS = 576
+GPSIMD_SLOTS = (96, 48)
 WIDE = 256
 TURNED = 256
 
@@ -106,7 +107,7 @@ def tile_moe_shr_lin_silu_kernel(tc, xT, w_words, w_scales, b, gate, offs, pos1,
                 lhsT_scale=scales_w[:, scale : scale + P],
             )
 
-        chunks = ((0, C), (C, 2 * C), (2 * C, 4 * C), (4 * C, 5 * C), (5 * C, S), (S, S + WIDE), (S + WIDE, S + T))
+        chunks = ((0, 2 * C), (2 * C, 4 * C), (4 * C, 5 * C), (5 * C, S), (S, S + WIDE), (S + WIDE, S + T))
         slot_chunks = len(chunks) - 2
         codes = [keep.tile([P, s1 - s0], U32, name=f"codes{s0}", align_bytes=64) for s0, s1 in chunks[:slot_chunks]]
         scales = [keep.tile([P, s1 - s0], U8, name=f"scales{s0}", align_bytes=64) for s0, s1 in chunks]
@@ -119,9 +120,18 @@ def tile_moe_shr_lin_silu_kernel(tc, xT, w_words, w_scales, b, gate, offs, pos1,
             window = tokens[:, table_at[u] : table_at[u] + width]
             nc.vector.tensor_copy(to, window.indirect(offs_t[:, s0 // LISTED : s1 // LISTED]))
 
-        def interleave(i, planes):
+        def interleave_on_scalar(i, c0, c1):
+            s0 = chunks[i][0]
             nc.scalar.copy(
-                grouped[i].bitcast(F32).rearrange("p (s u) -> p s u", u=2), planes.bitcast(F32).rearrange("p u s -> p s u")
+                grouped[i].bitcast(F32).rearrange("p (s u) -> p s u", u=2)[:, c0:c1],
+                picked[:, :, s0 + c0 : s0 + c1].bitcast(F32).rearrange("p u s -> p s u"),
+            )
+
+        def interleave_on_gpsimd(i, c0, c1):
+            s0 = chunks[i][0]
+            round_on_gpsimd(
+                grouped[i].bitcast(BF16).rearrange("p (s u e) -> p s u e", u=2, e=2)[:, c0:c1],
+                picked_tile[:].bitcast(BF16).rearrange("p (u s e) -> p s u e", u=2, e=2)[:, s0 + c0 : s0 + c1],
             )
 
         def quantise(i, c0, c1):
@@ -151,16 +161,11 @@ def tile_moe_shr_lin_silu_kernel(tc, xT, w_words, w_scales, b, gate, offs, pos1,
             )
         for i in range(slot_chunks):
             s0, s1 = chunks[i]
-            if i == 0:
-                pick_pairs(picked[:, 1, 0 : 2 * C], 1, 0, 2 * C, WINDOW)
-                round_on_gpsimd(
-                    grouped[0].bitcast(BF16).rearrange("p (s u e) -> p s u e", u=2, e=2),
-                    picked_tile[:].bitcast(BF16).rearrange("p (u s e) -> p s u e", u=2, e=2)[:, s0:s1],
-                )
-            else:
-                if i > 1:
-                    pick_pairs(picked[:, 1, s0:s1], 1, s0, s1, WINDOW)
-                interleave(i, picked[:, :, s0:s1])
+            pick_pairs(picked[:, 1, s0:s1], 1, s0, s1, WINDOW)
+            on_gpsimd = GPSIMD_SLOTS[i] if i < len(GPSIMD_SLOTS) else 0
+            if on_gpsimd:
+                interleave_on_gpsimd(i, 0, on_gpsimd)
+            interleave_on_scalar(i, on_gpsimd, s1 - s0)
             for c0 in range(0, s1 - s0, C):
                 quantise(i, c0, c0 + C)
         for (s0, s1), place in zip(chunks[slot_chunks:], ("last_grouped", f"grouped{4 * C}")):

import concourse.mybir as mybir
from concourse.masks import make_identity
from contextlib import ExitStack

K, T, E, C, N = 512, 384, 6, 128, 512
S = E * C
P = 128
ROW_TILES = N // P
SHARED = E

F32 = mybir.dt.float32
BF16 = mybir.dt.bfloat16
I32 = mybir.dt.int32
U32 = mybir.dt.uint32
U16 = mybir.dt.uint16
U8 = mybir.dt.uint8
FP8X4 = mybir.dt.float8_e4m3fn_x4
FP4X4 = mybir.dt.float4_e2m1fn_x4

MULT = mybir.AluOpType.mult
ADD = mybir.AluOpType.add
SILU = mybir.ActivationFunctionType.Silu
COPY = mybir.ActivationFunctionType.Copy

FLOPS = 2 * K * N * (S + T)
BYTES = 4 * K * T + (E + 1) * (K * N // 2 + K * N // 32) + 4 * N * (E + 1) + 2 * 4 * T + 2 * 128 * (48 + 24 + 24) + 4 * N * T

BANK = 512
LISTED = 16
WINDOW = 512
LONG_WINDOW = 896
VECTOR_CAST = 256
SCALAR_CAST = 192
VECTOR_SLOTS = 576
GPSIMD_SLOTS = (96, 48)
WIDE = 256
TURNED = 256


def tile_moe_shr_lin_silu_kernel(tc, xT, w_words, w_scales, b, gate, offs, pos1, pos2, out):
    nc = tc.nc
    with ExitStack() as ctx:
        lists = ctx.enter_context(tc.tile_pool(name="lists", bufs=1))
        keep = ctx.enter_context(tc.tile_pool(name="keep", bufs=1))
        psum = ctx.enter_context(tc.psum_pool(name="psum", bufs=1))

        offs_t = lists.tile([P, S // LISTED], U16, name="offs_t")
        pos1_t = lists.tile([P, T // LISTED], U16, name="pos1_t")
        pos2_t = lists.tile([P, T // LISTED], U16, name="pos2_t")

        tokens = keep.tile([P, 7 * T], U32, name="tokens", align_bytes=64)
        table_at = (2 * T, T)
        rows = tokens[:].bitcast(BF16)
        raw = tokens[:, 3 * T : 7 * T].bitcast(F32).rearrange("p (j t) -> p j t", j=4)
        words = [keep.tile([P, (E + 1) * N], U8, name=f"words{h}", align_bytes=64) for h in range(2)]
        scales_w = keep.tile([P, (E + 1) * N], U8, name="scales_w", align_bytes=64)
        bias = keep.tile([P, ROW_TILES, 8], F32, name="bias")
        table_load = keep.tile([P, 1], F32, name="table_load")
        gates = keep.tile([P, 2, T], F32, name="gates")

        x_rows = xT.rearrange("(p j) t -> p j t", j=4)
        nc.sync.dma_start(raw[:, 0:2], x_rows[:, 0:2])
        nc.sync.dma_start(offs_t[:], offs)
        nc.sync.dma_start(raw[:, 2:4], x_rows[:, 2:4])

        nc.gpsimd.memset(table_load[:], 0.0)
        nc.scalar.activation(table_load[:], table_load[:], SILU)
        nc.vector.memset(scales_w[:].bitcast(I32), 0)
        identity = keep.tile([P, P], F32, name="identity")
        make_identity(nc, identity[:])

        w_scales_i = w_scales.bitcast(I32)
        w_words_i = w_words.bitcast(I32)

        def load_words(h):
            nc.sync.dma_start(
                words[h][:].bitcast(I32).rearrange("p (e c) -> p e c", e=E + 1),
                w_words_i[:, 0, :, h * N // 4 : (h + 1) * N // 4].rearrange("e p c -> p e c"),
            )

        load_words(0)
        for r in range(4):
            nc.sync.dma_start(
                scales_w[:].bitcast(I32).rearrange("p (e c) -> p e c", e=E + 1)[r:P:32],
                w_scales_i[:, 0, r:16:4, :].rearrange("e q c -> q e c"),
            )
        nc.sync.dma_start(bias[:, :, 0 : E + 1], b.rearrange("(m p) e -> p m e", p=P))
        nc.sync.dma_start(pos1_t[:], pos1)
        nc.sync.dma_start(pos2_t[:], pos2)
        nc.sync.dma_start(gates[:], gate[:, 0:P, :].rearrange("r p t -> p r t"))
        load_words(1)

        def cast(engine_copy, u, t0, t1):
            engine_copy(
                tokens[:, table_at[u] + t0 : table_at[u] + t1].bitcast(BF16).rearrange("p (t e) -> p t e", e=2),
                raw[:, 2 * u : 2 * u + 2, t0:t1].rearrange("p e t -> p t e"),
            )

        def round_on_gpsimd(to, values):
            nc.gpsimd.tensor_scalar(to, values, 1.0, 0.0, MULT, ADD)

        def weights(e, m):
            word = e * N // 2 + m % 2 * P
            scale = e * N + m * P
            return dict(
                lhsT=words[m // 2][:, 2 * word : 2 * (word + P)].bitcast(FP4X4),
                lhsT_scale=scales_w[:, scale : scale + P],
            )

        chunks = ((0, 2 * C), (2 * C, 4 * C), (4 * C, 5 * C), (5 * C, S), (S, S + WIDE), (S + WIDE, S + T))
        slot_chunks = len(chunks) - 2
        codes = [keep.tile([P, s1 - s0], U32, name=f"codes{s0}", align_bytes=64) for s0, s1 in chunks[:slot_chunks]]
        scales = [keep.tile([P, s1 - s0], U8, name=f"scales{s0}", align_bytes=64) for s0, s1 in chunks]
        grouped = [
            keep.tile([P, 2 * (s1 - s0)], U32, name="last_grouped" if s1 == S else f"grouped{s0}", align_bytes=64)[:]
            for s0, s1 in chunks[:slot_chunks]
        ]

        def pick_pairs(to, u, s0, s1, width):
            window = tokens[:, table_at[u] : table_at[u] + width]
            nc.vector.tensor_copy(to, window.indirect(offs_t[:, s0 // LISTED : s1 // LISTED]))

        def interleave_on_scalar(i, c0, c1):
            s0 = chunks[i][0]
            nc.scalar.copy(
                grouped[i].bitcast(F32).rearrange("p (s u) -> p s u", u=2)[:, c0:c1],
                picked[:, :, s0 + c0 : s0 + c1].bitcast(F32).rearrange("p u s -> p s u"),
            )

        def interleave_on_gpsimd(i, c0, c1):
            s0 = chunks[i][0]
            round_on_gpsimd(
                grouped[i].bitcast(BF16).rearrange("p (s u e) -> p s u e", u=2, e=2)[:, c0:c1],
                picked_tile[:].bitcast(BF16).rearrange("p (u s e) -> p s u e", u=2, e=2)[:, s0 + c0 : s0 + c1],
            )

        def quantise(i, c0, c1):
            nc.vector.quantize_mx(
                out=codes[i][:, c0:c1].bitcast(FP8X4),
                scales=scales[i][:, c0:c1],
                in_=grouped[i][:, 2 * c0 : 2 * c1].bitcast(BF16),
            )

        cast(nc.vector.tensor_copy, 0, 0, VECTOR_CAST)
        cast(nc.scalar.copy, 0, VECTOR_CAST, T)
        nc.scalar.copy(rows[:, 0:T], raw[:, 0])
        nc.scalar.copy(rows[:, T + VECTOR_CAST : 2 * T], raw[:, 1, VECTOR_CAST:T])
        round_on_gpsimd(
            rows[:, T : T + VECTOR_CAST], rows[:, 2 * table_at[0] + 1 : 2 * (table_at[0] + VECTOR_CAST) : 2]
        )
        cast(nc.scalar.copy, 1, 0, SCALAR_CAST)
        cast(round_on_gpsimd, 1, SCALAR_CAST, T)
        picked_tile = keep.tile([P, 2 * S], U32, name="picked", align_bytes=64)
        picked = picked_tile[:].rearrange("p (u s) -> p u s", u=2)
        pick_pairs(picked[:, 0, 0:VECTOR_SLOTS], 0, 0, VECTOR_SLOTS, LONG_WINDOW)
        for e in range(2):
            nc.scalar.activation(
                picked[:, 0, VECTOR_SLOTS:S].bitcast(BF16)[:, e : 2 * (S - VECTOR_SLOTS) : 2],
                rows[:, e * T : e * T + WINDOW].indirect(offs_t[:, VECTOR_SLOTS // LISTED : S // LISTED]),
                COPY,
            )
        for i in range(slot_chunks):
            s0, s1 = chunks[i]
            pick_pairs(picked[:, 1, s0:s1], 1, s0, s1, WINDOW)
            on_gpsimd = GPSIMD_SLOTS[i] if i < len(GPSIMD_SLOTS) else 0
            if on_gpsimd:
                interleave_on_gpsimd(i, 0, on_gpsimd)
            interleave_on_scalar(i, on_gpsimd, s1 - s0)
            for c0 in range(0, s1 - s0, C):
                quantise(i, c0, c0 + C)
        for (s0, s1), place in zip(chunks[slot_chunks:], ("last_grouped", f"grouped{4 * C}")):
            grouped.append(keep.tile([P, 2 * (s1 - s0)], U32, name=place, align_bytes=64)[:])
            codes.append(keep.tile([P, s1 - s0], U32, name=f"codes{s0}", align_bytes=64))
            nc.vector.tensor_copy(
                grouped[-1].bitcast(I32).rearrange("p (t u) -> p t u", u=2),
                tokens[:, T : 3 * T].bitcast(I32).rearrange("p (u t) -> p t u", u=2)[:, s0 - S : s1 - S, ::-1],
            )
        quantise(slot_chunks + 1, 0, T - WIDE)
        quantise(slot_chunks, 0, WIDE)

        y = [keep.tile([P, S], F32, name=f"y{m}") for m in range(ROW_TILES)]

        def by_row_tile(name):
            early = [keep.tile([P, T], F32, name=f"{name}{m}")[:] for m in range(2)]
            late = keep.tile([P, 2 * T], F32, name=f"{name}_late")
            return early + [late[:, 0:T], late[:, T : 2 * T], late[:]]

        both_late = ROW_TILES
        ys = by_row_tile("ys")
        first = by_row_tile("first")
        second = by_row_tile("second")
        part = by_row_tile("part")
        total = by_row_tile("total")

        def bank(i):
            return psum.tile([P, BANK], F32, name=f"bank{i}")

        def product(sums, e, m, s0, s1):
            i = [j for j in range(len(chunks)) if chunks[j][0] <= s0 < chunks[j][1]][0]
            c0, c1 = s0 - chunks[i][0], s1 - chunks[i][0]
            nc.tensor.matmul_mx(
                out=sums,
                rhs=codes[i][:, c0:c1].bitcast(FP8X4),
                rhs_scale=scales[i][:, c0:c1],
                start=True,
                stop=True,
                **weights(e, m),
            )

        def routed(m, experts, i):
            sums = bank(i)
            for j, e in enumerate(experts):
                product(sums[:, j * C : (j + 1) * C], e, m, e * C, (e + 1) * C)
            for j, e in enumerate(experts):
                nc.scalar.activation(
                    y[m][:, e * C : (e + 1) * C],
                    sums[:, j * C : (j + 1) * C],
                    SILU,
                    bias=bias[:, m, e : e + 1],
                )

        def shared(m, i):
            sums = bank(i)
            for t0, t1 in ((0, WIDE), (WIDE, T)):
                product(sums[:, t0:t1], SHARED, m, S + t0, S + t1)
            nc.scalar.activation(ys[m], sums[:, 0:T], SILU, bias=bias[:, m, SHARED : SHARED + 1])

        def gathers(m):
            nc.vector.tensor_tensor(first[m], y[m][:].indirect(pos1_t[:]), gates[:, 0], MULT)
            nc.vector.tensor_tensor(second[m], y[m][:].indirect(pos2_t[:]), gates[:, 1], MULT)

        def turn_and_add(m, i, width):
            sums = bank(i)
            terms = (ys, first, second)
            for j, term in enumerate(terms):
                for t0 in range(0, width, P):
                    nc.tensor.matmul(
                        sums[:, t0 : t0 + P],
                        lhsT=term[m][:, t0 : t0 + P],
                        rhs=identity[:],
                        is_transpose=True,
                        start=j == 0 and t0 == 0,
                        stop=j == len(terms) - 1 and t0 + P == width,
                    )
            nc.scalar.copy(part[m][:, 0:width], sums[:, 0:width])

        def turn_back(m, i, width, queue):
            sums = bank(i)
            for t0 in range(0, width, P):
                nc.tensor.transpose(sums[:, t0 : t0 + P], part[m][:, t0 : t0 + P], identity[:])
            nc.scalar.copy(total[m][:, 0:width], sums[:, 0:width])
            queue.dma_start(out[m * P : (m + 1) * P, 0:width], total[m][:, 0:width])

        for e, i in enumerate((0, 1, 2, 3, 5, 6)):
            routed(0, (e,), i)
        routed(1, (5, 0), 4)
        routed(1, (1, 2), 3)
        routed(1, (3, 4), 5)
        gathers(0)
        shared(0, 6)
        routed(2, (5,), 0)
        routed(2, (0,), 3)
        routed(2, (1, 2, 3, 4), 4)
        gathers(1)
        shared(1, 0)
        routed(3, (5, 0, 1, 2), 6)
        turn_and_add(0, 3, T)
        routed(3, (3, 4), 4)
        gathers(2)
        shared(2, 0)
        shared(3, 6)
        turn_back(0, 1, T, nc.sync)
        turn_and_add(1, 2, T)
        turn_and_add(2, 5, TURNED)
        turn_back(1, 4, T, nc.scalar)
        turn_back(2, 7, TURNED, nc.scalar)

        def ends(views):
            return views[both_late].rearrange("p (m t) -> p m t", m=2)[:, :, TURNED:T]

        gathers(3)
        nc.vector.tensor_tensor(ends(part), ends(ys), ends(first), ADD)
        nc.vector.tensor_tensor(part[3][:, 0:TURNED], ys[3][:, 0:TURNED], first[3][:, 0:TURNED], ADD)
        nc.vector.tensor_tensor(ends(total), ends(part), ends(second), ADD)
        nc.sync.dma_start(out[2 * P : 4 * P, TURNED:T].rearrange("(m p) t -> p m t", p=P), ends(total))
        nc.vector.tensor_tensor(total[3][:, 0:TURNED], part[3][:, 0:TURNED], second[3][:, 0:TURNED], ADD)
        nc.sync.dma_start(out[3 * P : 4 * P, 0:TURNED], total[3][:, 0:TURNED])
